import numpy as np, ml_dtypes
CORES = [3,7,11,15,131,135,139,143]
N = 8
import mx_ref
BF = ml_dtypes.bfloat16
def gcols(t, e):
    v = np.concatenate([t.reshape(8, 16, -1, 4), np.zeros((8, 16, 1, 4), BF)], axis=2)
    return np.ascontiguousarray(np.stack([v[g][:, e[g]] for g in range(8)])).reshape(128, -1)
def tile(rs):
    return np.stack(rs, axis=2).reshape(128, -1).astype(BF)
def pick(q, e):
    c = np.concatenate([q[0].reshape(128, -1, 4), np.zeros((128, 1, 4), np.uint8)], axis=1); s = np.concatenate([q[1], np.ones((16, 1), np.uint8)], axis=1)
    return (np.ascontiguousarray(c[:, e].reshape(128, -1)), np.ascontiguousarray(s[:, e]))
def join(*qs):
    return (np.concatenate([q[0] for q in qs], axis=1), np.concatenate([q[1] for q in qs], axis=1))
def put(q, e, v):
    c, s = q[0].reshape(128, -1, 4).copy(), q[1].copy(); c[:, e] = v[0].reshape(128, -1, 4); s[:, e] = v[1]
    return (c.reshape(128, -1), s)
def pk(c, s):
    return (np.ascontiguousarray(c), mx_ref.live(s))
def emit(q):
    return q[0], q[1]
def packed(v, rng):
    q = [mx_ref.quantize(np.ascontiguousarray(v[r])) for r in range(N)]
    return np.stack([a for a, b in q]), np.stack([mx_ref.plane(b, rng) for a, b in q])
def values_of_codes():
    e, c = np.zeros((128, 128, 4), np.float32), np.zeros((128, 2, 4), np.uint8)
    e[np.arange(128), np.arange(128), 0] = 1
    c[:127, :, 0] = np.arange(256).reshape(2, 128).T[:127]
    return mx_ref.matmul(mx_ref.quantize(e.reshape(128, 512).astype(BF)), (c.reshape(128, 8), np.full((16, 2), 127, np.uint8))).T.reshape(-1).astype(np.float64)
CODE_VALUE, SCALE_VALUE = values_of_codes(), 2.0 ** (np.arange(256) - 127.0)
def decode(q):
    return (CODE_VALUE[q[0]].reshape(16, 8, -1, 4) * SCALE_VALUE[q[1]][:, None, :, None] + 0.0).reshape(128, -1).astype(np.float32)
def f(rng, *shape):
    return mx_ref.flush((rng.standard_normal(shape, dtype=np.float32) * np.exp2(rng.integers(-2, 3, shape[:-1] + (1,)))).astype(BF))
def wide(rng, *shape, cols=0):
    v = rng.standard_normal(shape, dtype=np.float32) * np.exp2(rng.integers(-12, 13, shape)).astype(np.float32)
    if cols: v *= np.repeat(np.exp2(rng.integers(-cols, cols + 1, shape[:-2] + (1, shape[-1] // 4))) * (rng.random(shape[:-2] + (1, shape[-1] // 4)) > 0.0625), 4, axis=-1).astype(np.float32)
    return mx_ref.flush(v.astype(BF))
C, S, K, W, M, R = 320, 40, 8, 2, 2, 3
def big(v):
    v = v.astype(np.float32)
    v[np.abs(v) < np.float32(2.0 ** -16)] = 0
    return v.astype(BF)
def numbers_of(rng):
    return {"x": big(f(rng, N, 128, 4 * C)), "u": np.array(f(rng, N, 128, 512)), "v": np.array(f(rng, N, 128, 512))}
def layers(rng):
    return big(f(rng, N, 128, 2048)).reshape(N, 8, 16, 4, 8, 16, 4)
def weights(rng, w):
    c, p = packed(np.ascontiguousarray(w).reshape(N, 128, 2048), rng)
    return {"wc": c, "ws": p}
def bare(u):
    u = u.reshape(N, 128, 128, 4)
    u[:, :, ::16] = 0
    u[:, :, 1::16] = 0
    return u
def setup_inputs(rng):
    return {**numbers_of(rng), **weights(rng, layers(rng))}
def setup_inputs_ties(rng):
    d = numbers_of(rng)
    o = rng.permutation(N)
    x = d["x"].reshape(N, 8, 16, C, 4)
    x[:, :, :2] = 0
    x[:, :, :2, :, 0] = rng.integers(0, 3, (N, 8, 2, C)).astype(np.float32).astype(BF)
    u = bare(d["u"])
    for r in range(N):
        for h in range(0, 128, 16):
            u[r, h, h, 0] = 0.0 if r == o[0] else -1.0 if r == o[1] else 1.0
            u[r, h + 1, h + 1, 0] = u[r, h, h, 0]
    w = layers(rng)
    w[:, :, :, :, :, :2] = 0
    return {"x": x.reshape(N, 128, 4 * C), "u": u.reshape(N, 128, 512), "v": d["v"], **weights(rng, w)}
def setup_inputs_near(rng):
    d = numbers_of(rng)
    x = d["x"].astype(np.float32).reshape(N, 8, 16, C, 4)
    x[:, :, 0] = 0
    x[:, :, 8:] = 0
    u = bare(d["u"])
    s = rng.integers(0, 16, (N, 8, 2, C))
    s = ((s[..., None] >> np.arange(4)) & 1) * np.exp2(np.arange(4) - 23.0)
    h = rng.permutation(8)
    for i in range(8):
        g, k, p = h[i], i // 2, 16 * h[i]
        a = 1.0 if k == 0 else 2.0 ** -30
        if k == 2: x[:, g, 8:10, :, :i - 3] = (1.0 + 0.125 * rng.integers(0, 8, (N, 2, C, i - 3))) * 2.0 ** -30
        else: x[:, g, 8:10] = s[:, g]
        if k < 2:
            x[:, g, 0, :, 0] = 1.0 - 2.0 * (i % 2)
            x[:, g, 11, :, 0] = 2.0 ** -10
        if k == 3:
            for r in range(N): x[r, g, 0, rng.permutation(C)[:2], 0] = np.array([2.0 ** 29, -2.0 ** 29])
        for j in range(2):
            u[:, p + 8 + j, p + j] = a
            if i == 5:
                u[:, p + 8 + j, p + j, 0] = 1.125 * a
                u[:, p + 8 + j, p + j, 1] = -a
            if k < 2:
                u[:, p, p + j, 0] = a
                u[:, p + 11, p + j, 0] = a
            if k == 3: u[:, p, p + j, 0] = 1.0
    w = layers(rng)
    for i in [0, 8, 9, 10, 11, 12, 13, 14, 15]:
        w[:, :, i] = 0
        w[:, :, :, :, :, i] = 0
    return {"x": x.reshape(N, 128, 4 * C).astype(BF), "u": u.reshape(N, 128, 512), "v": d["v"], **weights(rng, w)}
def setup_inputs_huge(rng):
    d = numbers_of(rng)
    e = int(rng.integers(N))
    c = (np.argsort(rng.random((N, C)), axis=1) % 2 * 2.0 - 1.0).reshape(N, 1, 1, C, 1)
    c[e] = 1.0
    c[(e + 1) % N] = np.minimum(c[(e + 1) % N], 0.5)
    c[(e - 1) % N] = -1.0
    x = (1.0 - 0.0625 * rng.integers(0, 3, (N, 8, 16, C, 4))) * 2.0 ** 30 * c
    u = bare(d["u"])
    u[:, :, ::16] = (2.0 ** 30 * np.where(rng.random((N, 128, 8, 4)) < 0.25, 0.875, 1.0)).astype(np.float32).astype(BF)
    u[:, :, 1::16] = (2.0 ** 30 * np.where(rng.random((N, 128, 8, 4)) < 0.5, 0.25, 1.0)).astype(np.float32).astype(BF)
    w = np.zeros((N, 128, 4, 128, 4), np.float32)
    i = np.arange(128)
    for b in range(4): w[:, i, b, i, b] = -1
    return {"x": x.astype(np.float32).reshape(N, 128, 4 * C).astype(BF), "u": u.reshape(N, 128, 512), "v": d["v"], **weights(rng, w.astype(BF))}
def setup_inputs_held(rng):
    d = numbers_of(rng)
    x = d["x"].astype(np.float32).reshape(N, 8, 16, C, 4)
    t = (N, 8, 8, C, 4)
    x[:, :, :2] = 0
    x[:, :, 8:] = (1.0 + (2 * rng.integers(0, 64, t) + 1) * 2.0 ** -7) * np.exp2(-1.0 * rng.integers(8, 15, t)) * rng.choice([-1.0, 1.0], t)
    x[:, :, 8, :, 0] = 1.96875 * rng.choice([-1.0, 1.0], (N, 8, C))
    n = np.argsort(rng.random((N, 8, C)), axis=2)
    m = C - 1 - n
    x[:, :, 0, :, :3] = np.stack([m & 7, m & 56, m & 448], axis=-1)
    turn, at = rng.integers(0, 4, (8, S)), rng.integers(0, 2, (8, S))
    g = np.arange(8)[:, None]
    for r in range(N):
        k = n[r] // K
        x[r, :, 1, :, 0] = np.where(n[r] % K == at[g, k], np.array([8.0, 0.0, 2.0, 3.0])[(r + turn[g, k]) % 4], 0.0)
    u = bare(d["u"])
    for h in range(0, 128, 16):
        u[:, h, h, :3] = 1.0
        u[:, h + 1, h + 1, 0] = 1.0
    w = layers(rng)
    w[:, :, 0] = 0
    w[:, :, :, :, :, :2] = 0
    w[:, :, :, :, :, 8:] = 0
    return {"x": x.reshape(N, 128, 4 * C).astype(BF), "u": u.reshape(N, 128, 512), "v": d["v"], **weights(rng, w)}
def setup_inputs_spread(rng):
    d = setup_inputs(rng)
    d["x"] = big(wide(rng, N, 128, 4 * C, cols=6))
    return d
def check_inputs(d):
    b = []
    for k in ("x", "u", "v"):
        a = np.abs(d[k].astype(np.float32))
        if not (np.isfinite(a).all() and ((a == 0) | (a >= 2.0 ** -30) & (a <= 2.0 ** 30)).all()): b.append("a value of " + k)
    none, least, most = [emit(mx_ref.quantize(np.full((128, 16), k, np.float32).astype(BF)))[1][0, 0] for k in (0.0, 2.0 ** -30, 2.0 ** 30)]
    for r in range(N):
        if ((d["wc"][r] == 0x7F) | (d["wc"][r] == 0xFF)).any(): b.append("wc: a code that is no number")
        s = mx_ref.live(d["ws"][r])
        if ((s != none) & ((s < least) | (s > most))).any(): b.append("ws: a scale out of range")
    return b
def reference(x, u, v, wc, ws):
    qu = [mx_ref.quantize(u[r]) for r in range(N)]
    lay = [pk(wc[r], ws[r]) for r in range(N)]
    now = [x[r] for r in range(N)]
    held = np.full((N, 8, S, K), -1)
    cursor = np.zeros((N, 8, S), np.int64)
    kept = [np.zeros((128, 0), BF) for r in range(N)]
    item = np.arange(K)
    for t in range(R):
        score = [mx_ref.matmul(qu[r], mx_ref.quantize(now[r])) for r in range(N)]
        if t == 0: order = np.stack([np.argsort(-(score[r][::16] + np.float32(0.0)), axis=1, kind="stable") for r in range(N)])
        made = []
        for r in range(N):
            e = (r - 1) % N
            k = np.argsort(held[r] >= 0, axis=2, kind="stable")[:, :, :W]
            n = (K * np.arange(S)[:, None] + k).reshape(8, S * W)
            q = mx_ref.quantize(gcols(now[e], np.take_along_axis(order[e], n, axis=1)))
            kept[r] = np.concatenate([kept[r], decode(q).astype(BF)], axis=1)
            theirs = mx_ref.matmul(qu[r], q)[1::16]
            own = np.take_along_axis(score[r][1::16], np.take_along_axis(order[r], n, axis=1), axis=1)
            np.put_along_axis(held[r], k, np.where(theirs < own, -1, S * W * t + np.arange(S * W)).reshape(8, S, W), axis=2)
            lead = np.argmin(np.concatenate([held[r], np.full((8, S, 1), -1)], axis=2) >= 0, axis=2)
            end = np.minimum(cursor[r] + M, lead)
            goes = (item >= cursor[r][:, :, None]) & (item < end[:, :, None])
            cursor[r] = end
            where = np.zeros((8, C), np.int64)
            np.put_along_axis(where, order[r], np.where(goes, C + held[r], order[r].reshape(8, S, K)).reshape(8, C), axis=1)
            other = gcols(np.concatenate([now[r], kept[r]], axis=1), where)
            z = ((now[r].astype(np.float32) + other.astype(np.float32)) * np.float32(0.5)).astype(BF)
            qz = mx_ref.quantize(z)
            made.append(tile([mx_ref.matmul(pick(lay[r], np.arange(128 * b, 128 * b + 128)), qz) * np.float32(0.03125) + z[:, b::4].astype(np.float32) for b in range(4)]))
        now = made
    y, sk = np.zeros((N, 128, C), np.float32), np.zeros((N, 8, C), np.float32)
    oc, osc = np.zeros((N, 128, 4 * C), np.uint8), np.zeros((N, 16, C), np.uint8)
    for r in range(N):
        q = mx_ref.quantize(now[r])
        y[r] = mx_ref.matmul(mx_ref.quantize(v[r]), q)
        sk[r] = held[r].reshape(8, C)
        oc[r], osc[r] = emit(q)
    return {"y": y, "sk": sk, "oc": oc, "osc": osc}

@@ -1,0 +1,638 @@
+from concourse.mybir import dt, AluOpType, ActivationFunctionType
+
+C, NT, R = 320, 80, 3
+H = float(2.0 ** 90)
+F32, BF, I32, U16, CODE, PL = "float32", "bfloat16", "int32", "uint16", "float8_e4m3fn_x4", "uint8"
+ACT_SLOTS = [19, 18, 17]
+
+
+def _sb(n, d):
+    return ("sbuf", [128, n], d)
+
+
+SCRATCH = {
+    "ps": ("psum", [128, 4096], F32),
+    "ut": _sb(512, BF), "vt": _sb(512, BF), "qu": _sb(128, CODE), "su": _sb(128, PL), "qp": _sb(256, CODE), "sp": _sb(256, PL),
+    "qv": _sb(128, CODE), "sv": _sb(128, PL), "qw": _sb(512, CODE), "sw": _sb(512, PL),
+    "gt": _sb(512, BF), "qg": _sb(128, CODE), "sg": _sb(128, PL),
+    "et": _sb(2048, BF), "qe": _sb(512, CODE), "se": _sb(512, PL), "zero": _sb(512, BF),
+    "cmp": _sb(5 * 1280, BF), "qc": _sb(5 * C, CODE), "scm": _sb(5 * C, PL), "sig": _sb(3 * C, BF), "junk": _sb(2048, BF),
+    "z0": _sb(1600, BF), "z1": _sb(1600, BF), "z2": _sb(1600, BF), "z3": _sb(1280, BF),
+    "x32": _sb(1280, BF), "z32": _sb(1280, BF), "qz": _sb(C, CODE), "sz": _sb(C, PL),
+    "qx0": _sb(400, CODE), "sx0": _sb(400, PL), "qx1": _sb(400, CODE), "sx1": _sb(400, PL),
+    "qx2": _sb(400, CODE), "sx2": _sb(400, PL), "qx3": _sb(C, CODE), "sx3": _sb(C, PL),
+    "tt": _sb(512, BF), "qt0": _sb(128, CODE), "st0": _sb(128, PL), "qt1": _sb(128, CODE), "st1": _sb(128, PL),
+    "qt2": _sb(128, CODE), "st2": _sb(128, PL),
+    "kept": _sb(960, BF), "xph": _sb(C, F32), "bl": _sb(C, BF),
+    "pi": _sb(16, I32), "pf": _sb(32, F32),
+    "uo": _sb(16, F32), "uo16": _sb(16, U16), "so": _sb(26, F32), "so16": _sb(26, U16),
+    "nm": _sb(C, BF), "blk": _sb(512, BF), "n4": _sb(400, BF), "r2": _sb(NT, BF), "c320": _sb(C, F32), "m16": _sb(20, F32),
+    "eq": _sb(C, BF), "ne": _sb(C, BF), "mm": _sb(C, BF), "k320": _sb(C, BF), "kr": _sb(C, BF), "kra": _sb(C, BF),
+    "me": _sb(400, BF), "k4": _sb(400, BF), "mt": _sb(NT, F32), "kc": _sb(NT, F32),
+    "vv": _sb(C, F32), "sc": _sb(C + 8, F32), "rs": _sb(C, F32), "rk16": _sb(20, U16), "orep": _sb(C, F32),
+    "lt0": _sb(16, BF), "miss": _sb(60, F32),
+    "g400": _sb(400, F32), "pp": _sb(400, F32), "dp": _sb(NT, F32),
+    "s1": _sb(C, F32), "bg": _sb(C, F32), "th": _sb(NT, F32), "acc": _sb(NT, F32), "cd": _sb(NT, F32),
+    "aa": _sb(5 * NT, F32), "kk": _sb(16 * NT, F32), "oo": _sb(19 * NT, F32), "ln": _sb(20 * 20, F32),
+    "w16": _sb(20, U16), "b16": _sb(20, U16), "x16": _sb(20, U16), "s16": _sb(20, U16), "o16": _sb(20, U16), "h16": _sb(20, U16),
+    "ls0": _sb(24, BF), "ls1": _sb(24, BF), "lr0": _sb(24, BF), "lr1": _sb(24, BF),
+    "tab": _sb(280, F32), "skr": _sb(C, F32), "yb": _sb(C, F32),
+}
+SEMAPHORES = ["sv_", "sa_", "sp_", "sg_", "dx0", "dx1", "du", "dwc", "dws", "dv", "ar0", "ar1", "ar2", "li0", "li1", "loc",
+              "o0", "o1", "o2", "o3", "o4", "o5", "o6", "o7"]
+ENG_SEM = {"V": "sv_", "A": "sa_", "P": "sp_", "G": "sg_"}
+
+
+def build(T, nxt, prv):
+    ops = []
+    OP = AluOpType
+    AF = ActivationFunctionType
+
+    def v(name, a=0, b=None, s=1):
+        return (name, a, SCRATCH[name][1][1] if b is None else b, s)
+
+    def ap(r):
+        return T[r[0]][:, r[1]:r[2]:r[3]] if r[3] != 1 else T[r[0]][:, r[1]:r[2]]
+
+    def bank(k, a, b):
+        return v("ps", 512 * k + a, 512 * k + b)
+
+    def add(eng, fn, rd, wr, sem=None, cnt=0, acc=False, kind="op"):
+        ops.append({"e": eng, "fn": fn, "rd": [r for r in rd if isinstance(r, tuple)], "wr": wr, "sem": sem, "cnt": cnt,
+                    "acc": acc, "kind": kind})
+
+    def sx(x):
+        return ap(x) if isinstance(x, tuple) else x
+
+    def src(x, off):
+        return ap(x) if off is None else ap(x).indirect(ap(off))
+
+    def ts(out, in0, s1, op0, s2=None, op1=None, off=None):
+        if op1 is None:
+            add("V", lambda q: q.tensor_scalar(ap(out), src(in0, off), sx(s1), None, op0), [in0, s1, off], [out])
+        else:
+            add("V", lambda q: q.tensor_scalar(ap(out), src(in0, off), sx(s1), sx(s2), op0, op1), [in0, s1, s2, off], [out])
+
+    def tt(out, in0, in1, op, off=None):
+        add("V", lambda q: q.tensor_tensor(ap(out), src(in0, off), ap(in1), op), [in0, in1, off], [out])
+
+    def cp(out, in_):
+        add("V", lambda q: q.tensor_copy(ap(out), ap(in_)), [in_], [out])
+
+    def ms(out, c):
+        add("V", lambda q: q.memset(ap(out), c), [], [out])
+
+    def scan(out, d0, d1, op0=OP.mult, op1=OP.add, init=0.0):
+        add("V", lambda q: q.tensor_tensor_scan(ap(out), ap(d0), ap(d1), init, op0, op1), [d0, d1], [out])
+
+    def quant(qc, qs, in_):
+        add("V", lambda q: q.quantize_mx(ap(qc), ap(qs), ap(in_)), [in_], [qc, qs])
+
+    def act(out, in_, func=AF.Identity, scale=None, bias=None, off=None, total=None):
+        kw = {}
+        if scale is not None:
+            kw["scale"] = sx(scale)
+        if bias is not None:
+            kw["bias"] = sx(bias)
+        if total is not None:
+            kw["accum_out"] = ap(total)
+        add("A", lambda q: q.activation(ap(out), src(in_, off), func, **kw), [in_, scale, bias, off],
+            [out] if total is None else [out, total])
+
+    def acp(out, in_):
+        act(out, in_, AF.Copy)
+
+    def fill(out, c):
+        act(out, v("nm", 0, len(range(out[1], out[2], out[3]))), scale=0.0, bias=c)
+
+    def mm(out, lq, ls, rq, rs_, start=True, stop=True):
+        add("P", lambda q: q.matmul_mx(ap(out), ap(lq), ap(ls), ap(rq), ap(rs_), start, stop), [lq, ls, rq, rs_], [out],
+            acc=not start)
+
+    def iota(out, pattern, base=0, ch=0):
+        if SCRATCH[out[0]][2] == I32:
+            add("G", lambda q: q.iota(ap(out), pattern, base, ch), [], [out])
+        else:
+            add("G", lambda q: q.iota(ap(out), pattern, base, ch, allow_small_or_imprecise_dtypes=True), [], [out])
+
+    def dma(eng, out, in_, rd, wr, sem):
+        add(eng, lambda q: q.dma_start(out, in_), rd, wr, sem=sem, cnt=16, kind="dma")
+
+    def send(out, in_, rd, to, sem):
+        add("G", lambda q: q.remote_dma(out, in_, T.sem[sem], T.sem["loc"], to[1], to[0], to[2]), rd, [], kind="send", cnt=to[3])
+
+    def arrive(wr, sem, cnt):
+        add("X", None, [], wr, sem=sem, cnt=cnt, kind="arrive")
+
+    def u8(r):
+        return ap(r).bitcast(dt.uint8)
+
+    def u32(r):
+        return ap(r).bitcast(dt.uint32)
+
+    def pick(to, off):
+        add("V", lambda q: q.tensor_copy(u32(to[0]), u32(v("qu")).indirect(ap(off))), [v("qu"), off], [to[0]])
+        add("A", lambda q: q.activation(ap(to[1]), ap(v("su")).indirect(ap(off)), AF.Copy), [v("su"), off], [to[1]])
+
+    def pf(k):
+        return v("pf", k, k + 1)
+
+    def ln(k):
+        return v("ln", 20 * k, 20 * k + 20)
+
+    def kk(k, j=None):
+        return v("kk", NT * k, NT * k + NT) if j is None else v("kk", NT * k + j, NT * k + NT, 4)
+
+    def oo(k, j=None):
+        return v("oo", NT * k, NT * k + NT) if j is None else v("oo", NT * k + j, NT * k + NT, 4)
+
+    def aa(k, j=None):
+        return v("aa", NT * k, NT * k + NT) if j is None else v("aa", NT * k + j, NT * k + NT, 4)
+
+    def pj(j):
+        return v("pp", NT * j + 3, NT * j + NT, 4)
+
+    def dpj(j):
+        return v("dp", 20 * j, 20 * j + 20)
+
+    Q_, GP, T_, QQ, I_, H_, KQ, HA, HB = [pf(k) for k in range(1, 10)]
+    Q1, SO, NI, DQ, RS, SA, SB, SC_, SD, IRS, IR0, H1, NH, NKQ, C0, C1, CDF, NEG = [pf(k) for k in range(10, 28)]
+    DUMP, DL, E0_, E2_, F_, TA, TD, TE, DN, DO, FA, FN, BASE1, BASE2, K01, K11, U0, U1, V0_, W0_ = [ln(k) for k in range(20)]
+    KC1, KC3, KC2, KK0, KX1, KX2, KK1, KH0, KH1, KOFF, KH2, KW1, KW2N, KW2, KS2, KE2 = range(16)
+    OW1, OC1, OX1, OX2, OC3, OOFF, OWN, OW2, OC2, OS2, OH, OX1N, OX2N, OWN2, OK0, OK1, OE2, OH0, OH1 = range(19)
+    Z = [v("z%d" % t, 0, 1280) for t in range(4)]
+    QX = [(v("qx%d" % t, 0, C), v("sx%d" % t, 0, C)) for t in range(4)]
+    UO = (v("qp", 0, 128), v("sp", 0, 128))
+    UR = (v("qp", 128, 256), v("sp", 128, 256))
+    hc = C // 2
+
+    dma("A", ap(v("ut")), T.u[:, :], [], [v("ut")], "du")
+    for k in range(2):
+        dma("S", ap(v("z0", 640 * k, 640 * k + 640)), T.x[:, 640 * k:640 * k + 640], [], [v("z0", 640 * k, 640 * k + 640)], "dx%d" % k)
+    dma("S", u8(v("qw")), T.wc[:, :], [v("z0", 1272, 1280)], [v("qw")], "dwc")
+    dma("S", ap(v("sw")), T.ws[:, :], [], [v("sw")], "dws")
+    dma("S", ap(v("vt")), T.v[:, :], [], [v("vt")], "dv")
+    iota(v("pi", 0, 1), [[0, 1]], 0, 1)
+    iota(v("uo"), [[1, 2], [16, 8]])
+    iota(v("nm"), [[0, 20], [1, 16]])
+    iota(v("blk"), [[1, 8], [0, 64]])
+    iota(v("m16"), [[16, 20]])
+    iota(v("r2"), [[0, 20], [1, 2], [0, 2]])
+    iota(v("so", 0, 6), [[64, 6]])
+    iota(v("so", 6, 26), [[1, 4], [64, 5]], 1)
+    iota(v("n4"), [[0, 100], [1, 4]])
+    iota(v("c320"), [[1, C]])
+    iota(v("zero"), [[0, 512]])
+    for b in range(4):
+        o = v("et", 512 * b, 512 * b + 512)
+        add("G", lambda q, o=o, b=b: q.affine_select(ap(o), ap(v("zero")), [[-1, 512]], OP.not_equal, 0.5, b, 4), [v("zero")], [o])
+    iota(v("tab", 40, 280), [[80, 3], [1, 2], [2, 40]])
+    P0 = v("pi", 0, 1)
+    ms(v("k320"), H)
+    for k, (sh, an) in enumerate([(0, 15), (4, 7), (0, 3), (2, 3), (2, 1), (3, 1), (0, 7), (1, 7), (0, 1)]):
+        if sh:
+            ts(v("pi", k + 1, k + 2), P0, sh, OP.logical_shift_right, an, OP.bitwise_and)
+        else:
+            ts(v("pi", k + 1, k + 2), P0, an, OP.bitwise_and)
+    cp(v("uo16"), v("uo"))
+    cp(v("pf", 1, 10), v("pi", 1, 10))
+    ms(v("k320", 0, C, 16), -H)
+    ms(v("sc", 0, 8), -H)
+    ts(Q1, Q_, 1.0, OP.add)
+    ts(v("eq"), v("nm"), Q_, OP.is_equal)
+    ts(v("kra"), v("nm"), Q1, OP.is_equal, 16383.0, OP.mult)
+    act(NI, I_, scale=-1.0, bias=1.0)
+    act(DQ, QQ, scale=4.0, bias=1280.0)
+    act(v("ne"), v("eq"), scale=-1.0, bias=1.0)
+    act(v("mm"), v("eq"), scale=2.0 * H, bias=-H)
+    ts(IR0, Q_, 15.0, OP.is_equal)
+    ts(SO, HA, 8.0, OP.mult, HB, OP.add)
+    ms(v("cmp", 4 * 80, 4 * 128), 0.0)
+    ms(v("miss", 0, 1), 0.0)
+    tt(v("kr"), v("kra"), v("ne"), OP.add)
+    act(RS, IR0, scale=1.0 - 2.0 ** -14, bias=2.0 ** -14)
+    act(IRS, IR0, scale=-16383.0, bias=16384.0)
+    act(H1, H_, bias=1.0)
+    act(NH, H_, scale=-1.0)
+    ts(v("gt"), v("blk"), GP, OP.is_equal)
+    quant(v("qu"), v("su"), v("ut"))
+    pick(UO, v("uo16", 0, 8))
+
+    for k in range(2):
+        a, b = hc * k, hc * k + hc
+        quant(v("qx0", a, b), v("sx0", a, b), v("z0", 4 * a, 4 * b))
+    mm(bank(6, 0, C), UO[0], UO[1], QX[0][0], QX[0][1])
+    mm(bank(7, 0, C), UO[0], UO[1], QX[0][0], QX[0][1])
+    pick(UR, v("uo16", 8, 16))
+    mm(bank(5, 0, C), UR[0], UR[1], QX[0][0], QX[0][1])
+    act(DUMP, v("m16"), bias=DQ)
+    act(SA, I_, scale=-640.0)
+    act(SB, I_, scale=320.0)
+    act(SC_, I_, scale=-320.0)
+    quant(v("qg"), v("sg"), v("gt"))
+    tt(v("vv", 256, C), bank(6, 256, C), v("mm", 256, C), OP.min)
+    tt(v("vv", 0, 256), bank(6, 0, 256), v("mm", 0, 256), OP.min)
+    scan(v("sc", 257, C + 1), v("k320", 256, C), v("vv", 256, C), OP.min, OP.max, -H)
+    scan(v("sc", 1, 257), v("k320", 0, 256), v("vv", 0, 256), OP.min, OP.max, -H)
+
+    def own(m):
+        return v("sc", 16 * m + 16, 16 * m + 17)
+
+    def row(m, a, b):
+        k = (m - 1) // 4
+        return v("cmp", 1280 * k + (m - 1) % 4 + 4 * a, 1280 * k + 4 * b, 4)
+
+    def width(k):
+        return min(64 * k + 80, C)
+
+    def low(m):
+        return 64 * ((m - 1) // 4) + 16
+
+    def miss(m):
+        return v("miss", m, m + 1)
+
+    for n, m in enumerate(ACT_SLOTS):
+        act(v("sig", C * n, C * n + C), bank(7, 0, C), AF.Sign, scale=-1.0, bias=own(m))
+    for n, m in enumerate(ACT_SLOTS):
+        e = min(16 * m + 17, C)
+        act(row(m, 0, low(m)), v("sig", C * n, C * n + low(m)), AF.Relu, total=v("miss", 40 + m, 41 + m))
+        act(row(m, low(m), e), v("sig", C * n + low(m), C * n + e), AF.Relu)
+        if e < C:
+            act(row(m, e, C), v("sig", C * n + e, C * n + C), AF.Sign, bias=1.0)
+    lo = min(ACT_SLOTS)
+    act(v("miss", lo, 20), v("miss", 40 + lo, 60), scale=-1.0, bias=float(low(19)))
+    tt(row(20, 0, C), bank(6, 0, C), v("sc", 0, C), OP.is_equal)
+    ts(v("lt0"), bank(6, 0, 16), own(0), OP.is_lt)
+    ms(v("cmp", 5120 + 3 + 4 * 16, 6400, 256), 0.0)
+    tt(row(20, 0, 16), row(20, 0, 16), v("lt0"), OP.add)
+
+    def count(k):
+        w = max(width(k), 128)
+        qc, qs = v("qc", C * k, C * k + w), v("scm", C * k, C * k + w)
+        quant(qc, qs, v("cmp", 1280 * k, 1280 * k + 4 * w))
+        mm(bank(0, 0, w), v("qg"), v("sg"), qc, qs, k == 4, k == 0)
+
+    used = [0]
+    for m in range(19, 0, -1):
+        if m in ACT_SLOTS:
+            continue
+        w = width((m - 1) // 4)
+        e = min(16 * m + 17, w)
+        ts(row(m, 0, e), bank(6, 0, e), own(m), OP.is_lt)
+        if e < w:
+            ts(row(m, e, w), bank(6, e, w), own(m), OP.is_le)
+        act(v("junk", used[0], used[0] + low(m)), row(m, 0, low(m)), scale=-1.0, bias=1.0, total=miss(m))
+        used[0] += low(m)
+        if m == 9:
+            count(4)
+            count(3)
+        if m == 7:
+            count(2)
+        if m == 4:
+            count(1)
+    ts(v("so16"), v("so"), SO, OP.add)
+    count(0)
+    act(v("miss", 20, 40), v("miss", 0, 20), scale=IRS)
+    ts(v("me"), v("n4"), QQ, OP.is_equal, 4.0, OP.mult)
+    act(v("s1"), bank(5, 0, C), AF.Copy)
+    act(v("k4"), v("n4"), AF.Sign)
+    for j, c in enumerate([0.0, 2.0, 1.0, H1]):
+        fill(v("kc", j, NT, 4), c)
+    act(v("mt"), v("r2"), AF.Abs, bias=NH)
+    fill(v("aa", 0, 5 * NT, 4), 0.0)
+    fill(v("aa", 3, 3 * NT, 4), 0.0)
+    act(v("mt"), v("mt"), scale=2.0 * H, bias=-H)
+    scan(v("rs"), v("kr"), bank(0, 0, C))
+    ms(v("tt", 320, 512), 0.0)
+    tt(TA, v("rs", 15, C, 16), v("miss", 20, 40), OP.add)
+    ts(v("rk16"), TA, RS, OP.mult)
+    add("V", lambda q: q.tensor_copy(ap(v("orep")).indirect(ap(v("rk16"))), ap(v("c320"))), [v("rk16"), v("c320")], [v("orep")])
+    tt(v("g400", 0, NT), v("orep"), v("me", 0, NT), OP.mult, off=v("so16", 0, 5))
+    scan(v("pp", 0, NT), v("k4", 0, NT), v("g400", 0, NT))
+    ts(v("w16"), pj(0), T_, OP.add)
+
+    def make_t(t):
+        s, f = (Z[0], 1.0) if t == 0 else (v("x32"), 2.0 ** -5)
+        act(v("tt", 160, 320), s, AF.Copy, scale=f, off=v("w16", 10, 20))
+        ts(v("tt", 0, 160), s, f, OP.mult, off=v("w16", 0, 10))
+        quant(v("qt%d" % t), v("st%d" % t), v("tt"))
+        a, b = v("qt%d" % t, 0, NT), v("st%d" % t, 0, NT)
+        send(u8(v("qx%d" % t, C, C + NT)), u8(a), [a], nxt, "ar%d" % t)
+        send(ap(v("sx%d" % t, C, C + NT)), ap(b), [b], nxt, "ar%d" % t)
+
+    def held_table(t, k0, k1, first, kh):
+        act(U0, k0, AF.Abs, bias=NKQ)
+        act(U1, k1, AF.Abs, bias=NKQ)
+        act(first, U0, AF.Relu, scale=-40.0 * (2 * t + 1), bias=40.0 * (2 * t + 1))
+        for j in (0, 2):
+            act(kk(kh, j), U1, AF.Relu, scale=-40.0 * (2 * t + 2), bias=40.0 * (2 * t + 2))
+
+    def thresholds():
+        act(v("bg"), v("s1"), AF.Copy, off=v("b16"))
+
+    def flight(t):
+        if t == 0:
+            ts(v("b16"), pj(0), 0.25, OP.mult)
+            thresholds()
+            act(v("xph"), Z[0], AF.Copy, scale=0.5, off=v("w16"))
+            quant(v("qe"), v("se"), v("et"))
+            tt(DL, pj(0), DUMP, OP.subtract)
+            ms(v("kk", NT * KH1 + 3, NT * KOFF + NT, 4), 0.0)
+            cp(kk(KOFF, 2), DUMP)
+            ts(kk(KOFF, 0), DL, I_, OP.mult)
+            ts(kk(KOFF, 1), DL, NI, OP.mult)
+            tt(v("th"), v("bg", 0, C, 4), v("mt"), OP.max)
+            tt(v("g400", NT, 400), v("orep"), v("me", NT, 400), OP.mult, off=v("so16", 6, 26))
+            ms(v("kk", NT * KC1 + 2, NT * KK0 + NT, 4), 0.0)
+            scan(v("pp", NT, 400), v("k4", NT, 400), v("g400", NT, 400))
+            ms(v("kk", NT * KX1 + 1, NT * KK1 + NT, 4), 0.0)
+            tt(v("dp"), v("pp", NT + 3, 400, 4), v("pp", 3, C, 4), OP.subtract)
+            act(BASE1, DUMP, bias=-960.0)
+            act(BASE2, DUMP, bias=-640.0)
+            fill(v("tab", 0, 40), -1.0)
+            act(kk(KH0, 3), v("m16"), scale=0.125, bias=H_)
+            act(NKQ, KQ, scale=-1.0)
+            act(SD, I_, scale=312.0, bias=-316.0)
+            act(NEG, I_, scale=-1.0)
+            ts(C0, KQ, 0.0, OP.is_equal, 40.0, OP.mult)
+            ts(C1, KQ, 1.0, OP.is_equal, 80.0, OP.mult)
+            quant(v("qv"), v("sv"), v("vt"))
+            acp(kk(KW1, 0), dpj(1))
+            act(kk(KW1, 1), dpj(0), scale=NI)
+            act(kk(KW1, 2), dpj(0), scale=I_)
+            acp(kk(KW1, 3), pj(0))
+            for k, col in ((KC1, [dpj(1), dpj(0), None, pj(0)]), (KX1, [dpj(2), None, dpj(1), pj(1)]),
+                           (KX2, [dpj(3), None, dpj(2), pj(2)]), (KC3, [dpj(3), dpj(2), None, pj(2)])):
+                for j, s in enumerate(col):
+                    if s is not None:
+                        acp(kk(k, j), s)
+            return
+        oc_ = OC1 if t == 1 else OC2
+        if t == 2:
+            scan(oo(OK0), aa(1), kk(KK0))
+            scan(oo(OK1), aa(1), kk(KK1))
+        act(v("xph"), v("x32"), AF.Copy, scale=2.0 ** -6, off=v("x16"))
+        if t == 2:
+            held_table(2, oo(OK0, 3), oo(OK1, 3), W0_, KH2)
+        for b in (2, 3):
+            ts(v("z%d" % t, b, 1280, 4), v("x32", b, 1280, 4), 2.0 ** -5, OP.mult)
+        tt(DL, oo(oc_, 3), DUMP, OP.subtract)
+        quant(QX[t][0], QX[t][1], Z[t])
+        mm(bank(5, 0, C), UR[0], UR[1], QX[t][0], QX[t][1])
+        if t == 1:
+            for k, j, c in ((KK0, 0, 1.0), (KK1, 0, 1.0), (KK1, 2, 1.0), (KH0, 0, C1), (KH0, 2, C1)):
+                fill(kk(k, j), c)
+        act(v("s1"), bank(5, 0, C), AF.Copy)
+        thresholds()
+        if t == 1:
+            tt(F_, aa(0, 3), aa(0, 2), OP.subtract)
+            tt(K01, aa(0, 2), aa(0, 1), OP.add)
+            tt(TA, aa(0, 3), aa(0, 1), OP.add)
+            ts(TD, F_, SC_, OP.mult, T_, OP.add)
+            ts(E2_, F_, I_, OP.mult, NI, OP.add)
+            ts(K11, TA, 1.0, OP.add)
+            tt(TD, TD, BASE1, OP.add)
+            tt(kk(KOFF, 1), E2_, DL, OP.mult)
+            scan(oo(OX1N), aa(3), kk(KX1))
+            cp(v("s16"), TD)
+            tt(kk(KOFF, 0), DL, kk(KOFF, 1), OP.subtract)
+            scan(oo(OX2N), aa(3), kk(KX2))
+            scan(oo(OX1), aa(0), kk(KX1))
+            scan(oo(OX2), aa(0), kk(KX2))
+            scan(oo(OC3), aa(0), kk(KC3))
+            tt(DN, oo(OX1N, 3), oo(OWN, 3), OP.subtract)
+            tt(kk(KW2N, 0), oo(OX2N, 3), oo(OX1N, 3), OP.subtract)
+            tt(DO, oo(OX1, 3), oo(OW1, 3), OP.subtract)
+            tt(kk(KW2, 0), oo(OX2, 3), oo(OX1, 3), OP.subtract)
+            tt(kk(KC2, 0), oo(OC3, 3), oo(OX1, 3), OP.subtract)
+            tt(kk(KC2, 1), oo(OX1, 3), oo(OC1, 3), OP.subtract)
+            tt(kk(KK0, 1), K11, K01, OP.subtract)
+            tt(v("th"), v("bg", 0, C, 4), v("mt"), OP.max)
+            held_table(1, K01, K11, V0_, KH1)
+        else:
+            scan(oo(OE2), aa(1), kk(KE2))
+            tt(E0_, FN, aa(1, 1), OP.mult)
+            tt(kk(KS2, 3), FA, BASE2, OP.add)
+            tt(TE, oo(OE2, 3), DL, OP.mult)
+            tt(TD, E0_, DL, OP.mult)
+            scan(oo(OS2), aa(1), kk(KS2))
+            tt(kk(KOFF, 0), DL, TE, OP.subtract)
+            tt(kk(KOFF, 2), TD, DUMP, OP.add)
+            tt(kk(KOFF, 1), TE, TD, OP.subtract)
+            ts(v("s16"), oo(OS2, 3), T_, OP.add)
+            tt(kk(KH2, 1), W0_, kk(KH2, 0), OP.subtract)
+            tt(kk(KH1, 1), V0_, kk(KH1, 0), OP.subtract)
+            scan(v("oo", NT * OH0, NT * OH1 + NT), v("aa", 0, 2 * NT), v("kk", NT * KH0, NT * KH1 + NT))
+            tt(kk(KH2, 3), oo(OH0, 3), oo(OH1, 3), OP.add)
+            tt(v("th"), v("bg", 0, C, 4), v("mt"), OP.max)
+
+    make_t(0)
+    for t in range(R):
+        flight(t)
+        arrive([v("qx%d" % t, C, C + NT), v("sx%d" % t, C, C + NT)], "ar%d" % t, 2 * prv[4])
+        mq, msc = v("qx%d" % t, 272, 400), v("sx%d" % t, 272, 400)
+        mm(bank(4, 0, 128), UR[0], UR[1], mq, msc)
+        for b in range(4):
+            mm(bank(b, 0, 128), v("qe", 128 * b, 128 * b + 128), v("se", 128 * b, 128 * b + 128), mq, msc)
+
+        def keep():
+            for b in range(4):
+                acp(v("kept", C * t + b, C * t + C, 4), bank(b, 48, 128))
+
+        if t:
+            keep()
+        tt(v("acc"), bank(4, 48, 128), v("th"), OP.is_ge)
+        scan(v("cd"), v("kc"), v("acc"))
+        code = v("cd", 3, NT, 4)
+        if t < R - 1:
+            cp(v("ls%d" % t, 0, 20), code)
+            send(ap(v("lr%d" % t, 0, 20)), ap(v("ls%d" % t, 0, 20)), [v("ls%d" % t, 0, 20)], prv, "li%d" % t)
+        ts(aa(t, 1), code, 3.0, OP.is_ge)
+        ts(aa(t, 2), code, 2.0, OP.is_ge)
+        scan(oo(OOFF), aa(t), kk(KOFF))
+        if t == 0:
+            for b in range(4):
+                tt(v("bl", b, C, 4), bank(b, 48, 128), v("xph", b, C, 4), OP.add)
+                if b == 0:
+                    ts(v("o16"), oo(OOFF, 2), T_, OP.add)
+            keep()
+            act(CDF, C1, scale=-1.0, bias=C0)
+            fill(kk(KH0, 1), CDF)
+        else:
+            ts(v("o16"), oo(OOFF, 2), T_, OP.add)
+            tt(v("bl"), v("kept", 0, C * t + C), v("xph"), OP.add, off=v("s16"))
+        if t == 1:
+            for kn, d, w in ((KW2, DO, oo(OW1, 3)), (KW2N, DN, oo(OWN, 3))):
+                act(kk(kn, 1), d, scale=NI)
+                act(kk(kn, 2), d, scale=I_)
+                acp(kk(kn, 3), w)
+            acp(kk(KC2, 3), oo(OC1, 3))
+            act(kk(KE2, 0), F_, scale=I_)
+            act(kk(KE2, 1), F_, scale=0.0, bias=NEG)
+            act(kk(KE2, 2), F_, scale=NEG, bias=I_)
+            acp(kk(KE2, 3), E2_)
+            acp(kk(KK0, 3), K01)
+            acp(kk(KK1, 3), K11)
+            act(kk(KS2, 0), F_, scale=SD)
+            act(kk(KS2, 1), F_, scale=SB, bias=SB)
+            act(kk(KS2, 2), F_, scale=SB, bias=SC_)
+        win = v("z%d" % t)
+        add("V", lambda q, win=win: q.tensor_copy(ap(win).indirect(ap(v("o16"))), ap(v("bl"))), [v("o16"), v("bl")], [win])
+        quant(v("qz"), v("sz"), Z[t])
+        for b in range(4):
+            act(v("z32", C * b, C * b + C), v("z%d" % t, b, 1280, 4), AF.Copy, scale=32.0)
+        for b in range(4):
+            mm(bank(b, 0, C), v("qw", 128 * b, 128 * b + 128), v("sw", 128 * b, 128 * b + 128), v("qz"), v("sz"))
+        ts(aa(t, 3), code, 1.0, OP.is_ge)
+        if t == R - 1:
+            scan(oo(OH), aa(2), kk(KH2))
+            cp(v("h16"), oo(OH, 3))
+        else:
+            kw, ow, kc_, oc_ = (KW1, OW1, KC1, OC1) if t == 0 else (KW2, OW2, KC2, OC2)
+            scan(oo(oc_), aa(t), kk(kc_))
+            scan(oo(ow), aa(t), kk(kw))
+            ts(v("x16"), oo(oc_, 3), T_, OP.add)
+            ts(v("b16"), oo(ow, 3), 0.25, OP.mult)
+            arrive([v("lr%d" % t, 0, 20)], "li%d" % t, nxt[4])
+        on, kn = (OWN, KW1) if t == 0 else (OWN2, KW2N)
+        for b in range(4):
+            if b == 2 and t < R - 1:
+                for j in range(1, 4):
+                    ts(aa(3 + t, j), v("lr%d" % t, 0, 20), float(4 - j), OP.is_ge)
+            if b == 3 and t < R - 1:
+                scan(oo(on), aa(3 + t), kk(kn))
+            tt(v("x32", b, 1280, 4), bank(b, 0, C), v("z32", C * b, C * b + C), OP.add)
+            if b < 2:
+                act(v("z%d" % (t + 1), b, 1280, 4), v("x32", b, 1280, 4), AF.Copy, scale=2.0 ** -5)
+        if t < R - 1:
+            ts(v("w16"), oo(on, 3), T_, OP.add)
+            make_t(t + 1)
+        if t == 1:
+            act(FA, F_, scale=SA)
+            act(FN, F_, scale=NI)
+
+    for b in (2, 3):
+        ts(v("z3", b, 1280, 4), v("x32", b, 1280, 4), 2.0 ** -5, OP.mult)
+    for k in range(2):
+        a, b = hc * k, hc * k + hc
+        quant(v("qx3", a, b), v("sx3", a, b), v("z3", 4 * a, 4 * b))
+        mm(bank(4 + k, 0, hc), v("qv"), v("sv"), v("qx3", a, b), v("sx3", a, b))
+    act(v("skr"), v("tab"), AF.Copy, off=v("h16"))
+    dma("S", T.oc[:, :], u8(v("qx3")), [v("qx3")], [], "o0")
+    for k in range(2):
+        cp(v("yb", hc * k, hc * k + hc), bank(4 + k, 0, hc))
+    dma("A", T.sk[:, :], T.skr[0:128:16, :], [v("skr")], [], "o1")
+    for k in range(2):
+        r = v("yb", hc * k, hc * k + hc)
+        dma("S", T.y[:, hc * k:hc * k + hc], ap(r), [r], [], "o%d" % (6 + k))
+    for k in range(4):
+        dma("A", T.osc[4 * k:4 * k + 4, :], T.sx3[32 * k:32 * k + 4, :], [v("sx3")], [], "o%d" % (2 + k))
+    return ops
+
+
+def meets(r, s):
+    if r[0] != s[0]:
+        return False
+    if r[0] == "ps":
+        return r[1] // 512 == s[1] // 512
+    if r[2] <= s[1] or s[2] <= r[1]:
+        return False
+    if r[3] == 1 and s[3] == 1:
+        return True
+    return len(set(range(r[1], r[2], r[3])) & set(range(s[1], s[2], s[3]))) > 0
+
+
+def order(ops):
+    seen = {}
+    deps = []
+    for n, o in enumerate(ops):
+        d = set()
+        for r, w in [(r, False) for r in o["rd"]] + [(r, True) for r in o["wr"]]:
+            for (m, s, w2) in seen.get(r[0], []):
+                other = ops[m]["e"] != o["e"]
+                if (w or w2 or (r[0] == "ps" and other)) and meets(r, s) and not (o["acc"] and not other):
+                    d.add(m)
+        for r, w in [(r, False) for r in o["rd"]] + [(r, True) for r in o["wr"]]:
+            seen.setdefault(r[0], []).append((n, r, w))
+        deps.append(d if o["kind"] != "arrive" else set())
+    return deps
+
+
+def plan(ops):
+    deps = order(ops)
+    place, cnt = {}, {}
+    for n, o in enumerate(ops):
+        if o["kind"] == "op":
+            cnt[o["e"]] = cnt.get(o["e"], 0) + 1
+            place[n] = (o["e"], cnt[o["e"]])
+        elif o["kind"] in ("dma", "arrive"):
+            place[n] = (o["sem"], 1)
+    know, at, waits = {}, [], []
+    for n, o in enumerate(ops):
+        k = know.setdefault(o["e"], {})
+        w = []
+        for m in sorted(deps[n], reverse=True):
+            key, c = place[m]
+            if k.get(key, 0) >= c:
+                continue
+            w.append(m)
+            k[key] = c
+            for key2, c2 in at[m].items():
+                if k.get(key2, 0) < c2:
+                    k[key2] = c2
+        waits.append(w)
+        at.append(dict(k))
+    return waits
+
+
+def rank_program(g, core, T, topo):
+    rank = T.rank_of(core)
+    if rank is None:
+        return
+    n = len(T.cores)
+    cn, cp_, cnn = T.cores[(rank + 1) % n], T.cores[(rank - 1) % n], T.cores[(rank + 2) % n]
+
+    def back(a, b, c):
+        return topo.mask(a, b) & topo.mask(a, c)
+
+    def bits(m):
+        return bin(m).count("1")
+
+    rn, pn = topo.addr(cn, core)
+    rp, pp_ = topo.addr(cp_, core)
+    nxt = (rn, pn, topo.mask(core, cn), bits(topo.mask(core, cn)), bits(back(cn, core, cnn)))
+    prv = (rp, pp_, back(core, cp_, cn), bits(back(core, cp_, cn)), bits(topo.mask(cp_, core)))
+    ops = build(T, nxt, prv)
+    waits = plan(ops)
+    needed = set(m for w in waits for m in w)
+    queue = {"V": g.vector, "A": g.scalar, "P": g.tensor, "G": g, "S": g.sync}
+    last = {}
+    for k, o in enumerate(ops):
+        if o["kind"] == "op":
+            last[o["e"]] = k
+    value, total, sent = {}, {}, 0
+    for k, o in enumerate(ops):
+        if o["kind"] == "op" and (k in needed or last[o["e"]] == k):
+            total[o["e"]] = total.get(o["e"], 0) + 1
+            value[k] = (ENG_SEM[o["e"]], total[o["e"]])
+        elif o["kind"] in ("dma", "arrive"):
+            value[k] = (o["sem"], o["cnt"])
+    for k, o in enumerate(ops):
+        if o["kind"] == "arrive":
+            continue
+        q = queue[o["e"]]
+        for m in waits[k]:
+            q.wait_ge(T.sem[value[m][0]], value[m][1])
+        ins = o["fn"](q)
+        if o["kind"] == "dma":
+            ins.then_inc(T.sem[o["sem"]], 16)
+        elif o["kind"] == "send":
+            sent += o["cnt"]
+        elif k in value:
+            ins.then_inc(T.sem[value[k][0]], 1)
+    g.wait_ge(T.sem["loc"], sent)
+    for e, c in total.items():
+        g.wait_ge(T.sem[ENG_SEM[e]], c)
+    for k, o in enumerate(ops):
+        if o["kind"] in ("dma", "arrive"):
+            g.wait_ge(T.sem[o["sem"]], o["cnt"])

@@ -2,8 +2,12 @@ from concourse.mybir import dt, AluOpType, ActivationFunctionType
 
 C, NT, R = 320, 80, 3
 H = float(2.0 ** 90)
+BIG = float(2.0 ** 80)
 F32, BF, I32, U16, CODE, PL = "float32", "bfloat16", "int32", "uint16", "float8_e4m3fn_x4", "uint8"
-ACT_SLOTS = [19, 18, 17]
+ACT_ROWS = [19, 18, 17]
+TILE_AT = {4: 0, 3: 320, 2: 576, 1: 832, 0: 960}
+TILE_W = {4: 320, 3: 256, 2: 256, 1: 128, 0: 128}
+ZW, ZB, ZM = 10240, 7680.0, 1280.0
 
 
 def _sb(n, d):
@@ -15,31 +19,31 @@ SCRATCH = {
     "ut": _sb(512, BF), "vt": _sb(512, BF), "qu": _sb(128, CODE), "su": _sb(128, PL), "qp": _sb(256, CODE), "sp": _sb(256, PL),
     "qv": _sb(128, CODE), "sv": _sb(128, PL), "qw": _sb(512, CODE), "sw": _sb(512, PL),
     "gt": _sb(512, BF), "qg": _sb(128, CODE), "sg": _sb(128, PL),
-    "et": _sb(2048, BF), "qe": _sb(512, CODE), "se": _sb(512, PL), "zero": _sb(512, BF),
-    "cmp": _sb(5 * 1280, BF), "qc": _sb(5 * C, CODE), "scm": _sb(5 * C, PL), "sig": _sb(3 * C, BF), "junk": _sb(2048, BF),
-    "z0": _sb(1600, BF), "z1": _sb(1600, BF), "z2": _sb(1600, BF), "z3": _sb(1280, BF),
+    "et": _sb(1056, BF), "qe": _sb(512, CODE), "se": _sb(512, PL), "zero": _sb(528, BF),
+    "cmp": _sb(4 * 1088, BF), "qc": _sb(1088, CODE), "scm": _sb(1088, PL), "sig": _sb(4 * C, BF), "junk": _sb(2304, BF),
+    "zz": _sb(3 * 1280 + ZW, BF),
     "x32": _sb(1280, BF), "z32": _sb(1280, BF), "qz": _sb(C, CODE), "sz": _sb(C, PL),
     "qx0": _sb(400, CODE), "sx0": _sb(400, PL), "qx1": _sb(400, CODE), "sx1": _sb(400, PL),
     "qx2": _sb(400, CODE), "sx2": _sb(400, PL), "qx3": _sb(C, CODE), "sx3": _sb(C, PL),
     "tt": _sb(512, BF), "qt0": _sb(128, CODE), "st0": _sb(128, PL), "qt1": _sb(128, CODE), "st1": _sb(128, PL),
     "qt2": _sb(128, CODE), "st2": _sb(128, PL),
     "kept": _sb(960, BF), "xph": _sb(C, F32), "bl": _sb(C, BF),
-    "pi": _sb(16, I32), "pf": _sb(32, F32),
-    "uo": _sb(16, F32), "uo16": _sb(16, U16), "so": _sb(26, F32), "so16": _sb(26, U16),
-    "nm": _sb(C, BF), "blk": _sb(512, BF), "n4": _sb(400, BF), "r2": _sb(NT, BF), "c320": _sb(C, F32), "m16": _sb(20, F32),
-    "eq": _sb(C, BF), "ne": _sb(C, BF), "mm": _sb(C, BF), "k320": _sb(C, BF), "kr": _sb(C, BF), "kra": _sb(C, BF),
-    "me": _sb(400, BF), "k4": _sb(400, BF), "mt": _sb(NT, F32), "kc": _sb(NT, F32),
-    "vv": _sb(C, F32), "sc": _sb(C + 8, F32), "rs": _sb(C, F32), "rk16": _sb(20, U16), "orep": _sb(C, F32),
-    "lt0": _sb(16, BF), "miss": _sb(60, F32),
+    "pi": _sb(16, I32), "pf": _sb(64, F32),
+    "uo": _sb(16, F32), "uo16": _sb(16, U16), "so": _sb(26, F32), "so16": _sb(26, U16), "q16": _sb(20, U16),
+    "nm": _sb(32, BF), "blk": _sb(512, BF), "n4": _sb(400, BF), "c320": _sb(C, F32), "m16": _sb(20, F32),
+    "p16": _sb(96, BF), "mm": _sb(C, BF), "k320": _sb(C, BF), "kr": _sb(C, BF), "kb": _sb(C, BF), "dsc": _sb(C, BF),
+    "me": _sb(400, BF), "k4": _sb(400, BF), "kc": _sb(NT, F32), "hi": _sb(NT, F32), "ko": _sb(NT, F32),
+    "vv": _sb(C, F32), "sc": _sb(C, F32), "rs": _sb(C, F32), "rk16": _sb(20, U16), "orep": _sb(C, F32),
+    "miss": _sb(60, F32),
     "g400": _sb(400, F32), "pp": _sb(400, F32), "dp": _sb(NT, F32),
-    "s1": _sb(C, F32), "bg": _sb(C, F32), "th": _sb(NT, F32), "acc": _sb(NT, F32), "cd": _sb(NT, F32),
-    "aa": _sb(5 * NT, F32), "kk": _sb(16 * NT, F32), "oo": _sb(19 * NT, F32), "ln": _sb(20 * 20, F32),
+    "s1": _sb(C, F32), "bg": _sb(C, F32), "th": _sb(NT, F32), "acc": _sb(2 * NT, F32), "cd": _sb(2 * NT, F32),
+    "aa": _sb(5 * NT, F32), "kk": _sb(14 * NT, F32), "oo": _sb(18 * NT, F32), "ln": _sb(20 * 20, F32),
     "w16": _sb(20, U16), "b16": _sb(20, U16), "x16": _sb(20, U16), "s16": _sb(20, U16), "o16": _sb(20, U16), "h16": _sb(20, U16),
     "ls0": _sb(24, BF), "ls1": _sb(24, BF), "lr0": _sb(24, BF), "lr1": _sb(24, BF),
     "tab": _sb(280, F32), "skr": _sb(C, F32), "yb": _sb(C, F32),
 }
 SEMAPHORES = ["sv_", "sa_", "sp_", "sg_", "dx0", "dx1", "du", "dwc", "dws", "dv", "ar0", "ar1", "ar2", "li0", "li1", "loc",
-              "o0", "o1", "o2", "o3", "o4", "o5", "o6", "o7"]
+              "o0", "o1", "o2", "o3", "o4", "o5", "o6", "o7", "o8"]
 ENG_SEM = {"V": "sv_", "A": "sa_", "P": "sp_", "G": "sg_"}
 
 
@@ -76,8 +80,8 @@ def build(T, nxt, prv):
     def tt(out, in0, in1, op, off=None):
         add("V", lambda q: q.tensor_tensor(ap(out), src(in0, off), ap(in1), op), [in0, in1, off], [out])
 
-    def cp(out, in_):
-        add("V", lambda q: q.tensor_copy(ap(out), ap(in_)), [in_], [out])
+    def cp(out, in_, off=None):
+        add("V", lambda q: q.tensor_copy(ap(out), src(in_, off)), [in_, off], [out])
 
     def ms(out, c):
         add("V", lambda q: q.memset(ap(out), c), [], [out])
@@ -103,7 +107,11 @@ def build(T, nxt, prv):
         act(out, in_, AF.Copy)
 
     def fill(out, c):
-        act(out, v("nm", 0, len(range(out[1], out[2], out[3]))), scale=0.0, bias=c)
+        act(out, v("k320", 0, len(range(out[1], out[2], out[3]))), scale=0.0, bias=c)
+
+    def affine(rows):
+        for o, i_, s, b in rows:
+            act(o, i_, scale=s, bias=b)
 
     def mm(out, lq, ls, rq, rs_, start=True, stop=True):
         add("P", lambda q: q.matmul_mx(ap(out), ap(lq), ap(ls), ap(rq), ap(rs_), start, stop), [lq, ls, rq, rs_], [out],
@@ -114,6 +122,9 @@ def build(T, nxt, prv):
             add("G", lambda q: q.iota(ap(out), pattern, base, ch), [], [out])
         else:
             add("G", lambda q: q.iota(ap(out), pattern, base, ch, allow_small_or_imprecise_dtypes=True), [], [out])
+
+    def whole(out, c):
+        iota(out, [[0, len(range(out[1], out[2], out[3]))]], c)
 
     def dma(eng, out, in_, rd, wr, sem):
         add(eng, lambda q: q.dma_start(out, in_), rd, wr, sem=sem, cnt=16, kind="dma")
@@ -134,20 +145,23 @@ def build(T, nxt, prv):
         add("V", lambda q: q.tensor_copy(u32(to[0]), u32(v("qu")).indirect(ap(off))), [v("qu"), off], [to[0]])
         add("A", lambda q: q.activation(ap(to[1]), ap(v("su")).indirect(ap(off)), AF.Copy), [v("su"), off], [to[1]])
 
-    def pf(k):
-        return v("pf", k, k + 1)
+    def pf(k, n=1):
+        return v("pf", k, k + n)
 
-    def ln(k):
-        return v("ln", 20 * k, 20 * k + 20)
+    def ln(k, n=1):
+        return v("ln", 20 * k, 20 * (k + n))
 
-    def kk(k, j=None):
-        return v("kk", NT * k, NT * k + NT) if j is None else v("kk", NT * k + j, NT * k + NT, 4)
+    def kk(k, j=None, n=1):
+        return v("kk", NT * k + (j or 0), NT * (k + n), 1 if j is None else 4)
 
-    def oo(k, j=None):
-        return v("oo", NT * k, NT * k + NT) if j is None else v("oo", NT * k + j, NT * k + NT, 4)
+    def oo(k, j=None, n=1):
+        return v("oo", NT * k + (j or 0), NT * (k + n), 1 if j is None else 4)
 
-    def aa(k, j=None):
-        return v("aa", NT * k, NT * k + NT) if j is None else v("aa", NT * k + j, NT * k + NT, 4)
+    def aa(k, j=None, n=1):
+        return v("aa", NT * k + (j or 0), NT * (k + n), 1 if j is None else 4)
+
+    def four(name, j):
+        return v(name, j, NT, 4)
 
     def pj(j):
         return v("pp", NT * j + 3, NT * j + NT, 4)
@@ -155,12 +169,18 @@ def build(T, nxt, prv):
     def dpj(j):
         return v("dp", 20 * j, 20 * j + 20)
 
-    Q_, GP, T_, QQ, I_, H_, KQ, HA, HB = [pf(k) for k in range(1, 10)]
-    Q1, SO, NI, DQ, RS, SA, SB, SC_, SD, IRS, IR0, H1, NH, NKQ, C0, C1, CDF, NEG = [pf(k) for k in range(10, 28)]
-    DUMP, DL, E0_, E2_, F_, TA, TD, TE, DN, DO, FA, FN, BASE1, BASE2, K01, K11, U0, U1, V0_, W0_ = [ln(k) for k in range(20)]
-    KC1, KC3, KC2, KK0, KX1, KX2, KK1, KH0, KH1, KOFF, KH2, KW1, KW2N, KW2, KS2, KE2 = range(16)
-    OW1, OC1, OX1, OX2, OC3, OOFF, OWN, OW2, OC2, OS2, OH, OX1N, OX2N, OWN2, OK0, OK1, OE2, OH0, OH1 = range(19)
-    Z = [v("z%d" % t, 0, 1280) for t in range(4)]
+    def z(t, a=0, b=1280, s=1):
+        return v("zz", 1280 * (3 - t) + a, 1280 * (3 - t) + b, s)
+
+    Q_, GP, T_, I_, H_, HB = [pf(k) for k in range(1, 7)]
+    (QQ, KQ, Q1, SO, NI, RS, SB, SC_, SD, IRS, IR0, CQ, C0, C1, CDF, S1K, B1K, S3K, B3K, CM, CA, BH, BN,
+     TH1) = [pf(k) for k in range(8, 32)]
+    TH = {c: pf(31 + c) for c in (1, 2, 3)}
+    MS, MB = [pf(36 + j) for j in range(4)], [pf(40 + j) for j in range(4)]
+    YY, YI, F_, TA, TD, XX, D1, LB, DN, DO, K01, K11, U0, U1, V0_, W0_ = [ln(k) for k in range(16)]
+    KC1, KC3, KC2, KK0, KX1, KX2, KK1, KH0, KH1, KH2, KW1, KW2N, KW2, KD2 = range(14)
+    OWN, OW1, OX1N, OX1, OX2N, OX2, OC1, OC3, OW2, OC2, OD2, OH, OWN2, OK0, OK1, OH0, OH1 = range(17)
+    AN0, A0, A1, A2, AN1 = range(5)
     QX = [(v("qx%d" % t, 0, C), v("sx%d" % t, 0, C)) for t in range(4)]
     UO = (v("qp", 0, 128), v("sp", 0, 128))
     UR = (v("qp", 128, 256), v("sp", 128, 256))
@@ -168,267 +188,264 @@ def build(T, nxt, prv):
 
     dma("A", ap(v("ut")), T.u[:, :], [], [v("ut")], "du")
     for k in range(2):
-        dma("S", ap(v("z0", 640 * k, 640 * k + 640)), T.x[:, 640 * k:640 * k + 640], [], [v("z0", 640 * k, 640 * k + 640)], "dx%d" % k)
-    dma("S", u8(v("qw")), T.wc[:, :], [v("z0", 1272, 1280)], [v("qw")], "dwc")
+        dma("S", ap(z(0, 640 * k, 640 * k + 640)), T.x[:, 640 * k:640 * k + 640], [], [z(0, 640 * k, 640 * k + 640)], "dx%d" % k)
+    dma("S", u8(v("qw")), T.wc[:, :], [z(0, 1272, 1280)], [v("qw")], "dwc")
     dma("S", ap(v("sw")), T.ws[:, :], [], [v("sw")], "dws")
     dma("S", ap(v("vt")), T.v[:, :], [], [v("vt")], "dv")
     iota(v("pi", 0, 1), [[0, 1]], 0, 1)
-    iota(v("uo"), [[1, 2], [16, 8]])
-    iota(v("nm"), [[0, 20], [1, 16]])
-    iota(v("blk"), [[1, 8], [0, 64]])
+    iota(v("nm", 0, 16), [[1, 16]])
     iota(v("m16"), [[16, 20]])
-    iota(v("r2"), [[0, 20], [1, 2], [0, 2]])
+    iota(v("uo"), [[1, 2], [16, 8]])
+    iota(v("blk"), [[1, 8], [0, 64]])
+    iota(v("n4"), [[0, 100], [1, 4]])
     iota(v("so", 0, 6), [[64, 6]])
     iota(v("so", 6, 26), [[1, 4], [64, 5]], 1)
-    iota(v("n4"), [[0, 100], [1, 4]])
     iota(v("c320"), [[1, C]])
-    iota(v("zero"), [[0, 512]])
-    for b in range(4):
-        o = v("et", 512 * b, 512 * b + 512)
-        add("G", lambda q, o=o, b=b: q.affine_select(ap(o), ap(v("zero")), [[-1, 512]], OP.not_equal, 0.5, b, 4), [v("zero")], [o])
-    iota(v("tab", 40, 280), [[80, 3], [1, 2], [2, 40]])
+    iota(v("zero"), [[0, 528]])
+    for e in range(2):
+        o = v("et", 528 * e, 528 * e + 514)
+        add("G", lambda q, o=o, e=e: q.affine_select(ap(o), ap(v("zero", 0, 514)), [[-1, 514]], OP.not_equal, 0.5, 2 + e, 4),
+            [v("zero")], [o])
+    iota(v("kc"), [[0, 20], [2, 4]])
+    whole(four("ko", 0), 0)
+    whole(v("aa", 0, 5 * NT, 4), 0)
+    whole(kk(KC1, 2, 4), 0)
+    whole(kk(KX1, 1, 3), 0)
     P0 = v("pi", 0, 1)
-    ms(v("k320"), H)
-    for k, (sh, an) in enumerate([(0, 15), (4, 7), (0, 3), (2, 3), (2, 1), (3, 1), (0, 7), (1, 7), (0, 1)]):
+
+    def bits(k, sh, an):
         if sh:
-            ts(v("pi", k + 1, k + 2), P0, sh, OP.logical_shift_right, an, OP.bitwise_and)
+            ts(v("pi", k, k + 1), P0, sh, OP.logical_shift_right, an, OP.bitwise_and)
         else:
-            ts(v("pi", k + 1, k + 2), P0, an, OP.bitwise_and)
-    cp(v("uo16"), v("uo"))
-    cp(v("pf", 1, 10), v("pi", 1, 10))
+            ts(v("pi", k, k + 1), P0, an, OP.bitwise_and)
+
+    def beyond(k):
+        return v("cmp", 4 * (TILE_AT[k] + 64 * k + 16), 4 * (TILE_AT[k] + TILE_W[k]))
+
+    NM, EQ, KA, MM, KR = v("nm", 0, 16), v("p16", 0, 16), v("p16", 16, 32), v("p16", 32, 48), v("p16", 64, 80)
+    ms(v("k320"), H)
+    bits(1, 0, 15)
+    bits(2, 4, 7)
     ms(v("k320", 0, C, 16), -H)
-    ms(v("sc", 0, 8), -H)
+    cp(v("pf", 1, 3), v("pi", 1, 3))
+    for k in (4, 3, 1):
+        fill(beyond(k), 0.0)
+    for k, (sh, an) in enumerate([(0, 3), (2, 1), (3, 1), (0, 1)]):
+        bits(k + 3, sh, an)
+    ts(EQ, NM, Q_, OP.is_equal)
     ts(Q1, Q_, 1.0, OP.add)
-    ts(v("eq"), v("nm"), Q_, OP.is_equal)
-    ts(v("kra"), v("nm"), Q1, OP.is_equal, 16383.0, OP.mult)
-    act(NI, I_, scale=-1.0, bias=1.0)
-    act(DQ, QQ, scale=4.0, bias=1280.0)
-    act(v("ne"), v("eq"), scale=-1.0, bias=1.0)
-    act(v("mm"), v("eq"), scale=2.0 * H, bias=-H)
+    ts(v("q16"), v("m16"), 0.0, OP.mult, Q_, OP.add)
+    cp(v("pf", 3, 7), v("pi", 3, 7))
+    ts(MM, EQ, 2.0 * H, OP.mult, -H, OP.add)
+    ts(KA, NM, Q1, OP.is_equal, 16383.0, OP.mult)
+    cp(v("uo16"), v("uo"))
     ts(IR0, Q_, 15.0, OP.is_equal)
-    ts(SO, HA, 8.0, OP.mult, HB, OP.add)
-    ms(v("cmp", 4 * 80, 4 * 128), 0.0)
+    act(v("mm"), MM, AF.Copy, off=v("q16"))
+    tt(KR, KA, EQ, OP.subtract)
+    ms(beyond(2), 0.0)
+    ms(beyond(0), 0.0)
     ms(v("miss", 0, 1), 0.0)
-    tt(v("kr"), v("kra"), v("ne"), OP.add)
-    act(RS, IR0, scale=1.0 - 2.0 ** -14, bias=2.0 ** -14)
-    act(IRS, IR0, scale=-16383.0, bias=16384.0)
-    act(H1, H_, bias=1.0)
-    act(NH, H_, scale=-1.0)
-    ts(v("gt"), v("blk"), GP, OP.is_equal)
+    act(v("kb"), v("k320"), scale=0.5 / H, bias=0.5)
     quant(v("qu"), v("su"), v("ut"))
     pick(UO, v("uo16", 0, 8))
+    act(v("kr"), KR, bias=1.0, off=v("q16"))
+    affine([(IRS, IR0, -16383.0, 16384.0), (RS, IR0, 1.0 - 2.0 ** -14, 2.0 ** -14), (CQ, Q_, -1.0, 15.0),
+            (QQ, H_, 2.0, I_), (KQ, H_, -8.0, Q_), (SO, HB, -0.75, Q_)])
 
     for k in range(2):
         a, b = hc * k, hc * k + hc
-        quant(v("qx0", a, b), v("sx0", a, b), v("z0", 4 * a, 4 * b))
+        quant(v("qx0", a, b), v("sx0", a, b), z(0, 4 * a, 4 * b))
     mm(bank(6, 0, C), UO[0], UO[1], QX[0][0], QX[0][1])
     mm(bank(7, 0, C), UO[0], UO[1], QX[0][0], QX[0][1])
     pick(UR, v("uo16", 8, 16))
     mm(bank(5, 0, C), UR[0], UR[1], QX[0][0], QX[0][1])
-    act(DUMP, v("m16"), bias=DQ)
-    act(SA, I_, scale=-640.0)
-    act(SB, I_, scale=320.0)
-    act(SC_, I_, scale=-320.0)
-    quant(v("qg"), v("sg"), v("gt"))
-    tt(v("vv", 256, C), bank(6, 256, C), v("mm", 256, C), OP.min)
-    tt(v("vv", 0, 256), bank(6, 0, 256), v("mm", 0, 256), OP.min)
-    scan(v("sc", 257, C + 1), v("k320", 256, C), v("vv", 256, C), OP.min, OP.max, -H)
-    scan(v("sc", 1, 257), v("k320", 0, 256), v("vv", 0, 256), OP.min, OP.max, -H)
+    ts(v("gt"), v("blk"), GP, OP.is_equal)
 
     def own(m):
-        return v("sc", 16 * m + 16, 16 * m + 17)
+        return v("sc", 16 * m + 15, 16 * m + 16)
 
-    def row(m, a, b):
-        k = (m - 1) // 4
-        return v("cmp", 1280 * k + (m - 1) % 4 + 4 * a, 1280 * k + 4 * b, 4)
-
-    def width(k):
-        return min(64 * k + 80, C)
-
-    def low(m):
-        return 64 * ((m - 1) // 4) + 16
+    def row(m, e):
+        a = 4 * TILE_AT[(m - 1) // 4]
+        return v("cmp", a + (m - 1) % 4, a + 4 * e, 4)
 
     def miss(m):
         return v("miss", m, m + 1)
 
-    for n, m in enumerate(ACT_SLOTS):
-        act(v("sig", C * n, C * n + C), bank(7, 0, C), AF.Sign, scale=-1.0, bias=own(m))
-    for n, m in enumerate(ACT_SLOTS):
-        e = min(16 * m + 17, C)
-        act(row(m, 0, low(m)), v("sig", C * n, C * n + low(m)), AF.Relu, total=v("miss", 40 + m, 41 + m))
-        act(row(m, low(m), e), v("sig", C * n + low(m), C * n + e), AF.Relu)
-        if e < C:
-            act(row(m, e, C), v("sig", C * n + e, C * n + C), AF.Sign, bias=1.0)
-    lo = min(ACT_SLOTS)
-    act(v("miss", lo, 20), v("miss", 40 + lo, 60), scale=-1.0, bias=float(low(19)))
-    tt(row(20, 0, C), bank(6, 0, C), v("sc", 0, C), OP.is_equal)
-    ts(v("lt0"), bank(6, 0, 16), own(0), OP.is_lt)
-    ms(v("cmp", 5120 + 3 + 4 * 16, 6400, 256), 0.0)
-    tt(row(20, 0, 16), row(20, 0, 16), v("lt0"), OP.add)
+    def below(m):
+        ts(row(m, 16 * m), bank(6, 0, 16 * m), own(m), OP.is_lt)
+        a = 8 * m * (m - 1)
+        act(v("junk", a, a + 16 * m), row(m, 16 * m), scale=IRS, total=miss(m))
 
     def count(k):
-        w = max(width(k), 128)
-        qc, qs = v("qc", C * k, C * k + w), v("scm", C * k, C * k + w)
-        quant(qc, qs, v("cmp", 1280 * k, 1280 * k + 4 * w))
-        mm(bank(0, 0, w), v("qg"), v("sg"), qc, qs, k == 4, k == 0)
+        a, w = TILE_AT[k], TILE_W[k]
+        quant(v("qc", a, a + w), v("scm", a, a + w), v("cmp", 4 * a, 4 * (a + w)))
+        if k == 4:
+            mm(bank(0, 0, 192), v("qg"), v("sg"), v("qc", 128, C), v("scm", 128, C), True, False)
+            a3 = TILE_AT[3] + 128
+            mm(bank(0, 0, 128), v("qg"), v("sg"), v("qc", a3, a3 + 128), v("scm", a3, a3 + 128), False, False)
+        if k == 2:
+            mm(bank(0, 0, 128), v("qg"), v("sg"), v("qc", a + 128, a + w), v("scm", a + 128, a + w), False, True)
+        mm(bank(1, 0, 128), v("qg"), v("sg"), v("qc", a, a + 128), v("scm", a, a + 128), k == 3, k == 0)
 
-    used = [0]
-    for m in range(19, 0, -1):
-        if m in ACT_SLOTS:
-            continue
-        w = width((m - 1) // 4)
-        e = min(16 * m + 17, w)
-        ts(row(m, 0, e), bank(6, 0, e), own(m), OP.is_lt)
-        if e < w:
-            ts(row(m, e, w), bank(6, e, w), own(m), OP.is_le)
-        act(v("junk", used[0], used[0] + low(m)), row(m, 0, low(m)), scale=-1.0, bias=1.0, total=miss(m))
-        used[0] += low(m)
-        if m == 9:
-            count(4)
-            count(3)
-        if m == 7:
-            count(2)
-        if m == 4:
-            count(1)
-    ts(v("so16"), v("so"), SO, OP.add)
+    tt(v("vv", 256, C), bank(6, 256, C), v("mm", 256, C), OP.min)
+    quant(v("qg"), v("sg"), v("gt"))
+    scan(v("sc", 256, C), v("k320", 256, C), v("vv", 256, C), OP.min, OP.max, -H)
+    tt(v("vv", 0, 256), bank(6, 0, 256), v("mm", 0, 256), OP.min)
+    nr = len(ACT_ROWS)
+    for n in range(nr + 1):
+        if n < nr:
+            m = ACT_ROWS[n]
+            act(v("sig", C * n, C * n + 16 * m), bank(7, 0, 16 * m), AF.Sign, scale=-1.0, bias=own(m))
+        if n:
+            m = ACT_ROWS[n - 1]
+            act(row(m, 16 * m), v("sig", C * (n - 1), C * (n - 1) + 16 * m), AF.Relu, total=v("miss", 40 + m, 41 + m))
+    lo = min(ACT_ROWS)
+    below(16)
+    act(v("miss", lo, 20), v("miss", 40 + lo, 60), scale=IRS)
+    scan(v("sc", 0, 256), v("k320", 0, 256), v("vv", 0, 256), OP.min, OP.max, -H)
+    ts(C0, KQ, 0.0, OP.is_equal, 40.0, OP.mult)
+    below(15)
+    tt(row(20, C), bank(6, 0, C), v("sc"), OP.is_le)
+    below(14)
+    scan(v("dsc"), v("kb"), row(20, C))
+    below(13)
+    tt(YY, v("m16"), v("dsc", 15, C, 16), OP.subtract)
+    below(12)
+    count(3)
+    below(11)
+    below(10)
+    act(YI, YY, scale=IRS)
+    below(9)
+    count(4)
+    below(8)
+    count(2)
+    for m in (7, 6, 5, 4):
+        below(m)
+    count(1)
+    for m in (3, 2, 1):
+        below(m)
+    scan(v("rs", 128, C), v("kr", 128, C), bank(0, 0, 192))
     count(0)
-    act(v("miss", 20, 40), v("miss", 0, 20), scale=IRS)
+    act(SO, SO, scale=4.0)
+    act(v("k4", 0, NT), v("n4", 0, NT), AF.Sign)
     ts(v("me"), v("n4"), QQ, OP.is_equal, 4.0, OP.mult)
-    act(v("s1"), bank(5, 0, C), AF.Copy)
-    act(v("k4"), v("n4"), AF.Sign)
-    for j, c in enumerate([0.0, 2.0, 1.0, H1]):
-        fill(v("kc", j, NT, 4), c)
-    act(v("mt"), v("r2"), AF.Abs, bias=NH)
-    fill(v("aa", 0, 5 * NT, 4), 0.0)
-    fill(v("aa", 3, 3 * NT, 4), 0.0)
-    act(v("mt"), v("mt"), scale=2.0 * H, bias=-H)
-    scan(v("rs"), v("kr"), bank(0, 0, C))
-    ms(v("tt", 320, 512), 0.0)
-    tt(TA, v("rs", 15, C, 16), v("miss", 20, 40), OP.add)
-    ts(v("rk16"), TA, RS, OP.mult)
+    tt(XX, YI, v("miss", 0, 20), OP.subtract)
+    scan(v("rs", 0, 128), v("kr", 0, 128), bank(1, 0, 128))
+    ts(v("so16"), v("so"), SO, OP.add)
+    tt(TA, v("rs", 15, C, 16), XX, OP.add)
+    ts(C1, KQ, 1.0, OP.is_equal, 80.0, OP.mult)
+    ts(v("rk16"), TA, RS, OP.mult, CQ, OP.add)
     add("V", lambda q: q.tensor_copy(ap(v("orep")).indirect(ap(v("rk16"))), ap(v("c320"))), [v("rk16"), v("c320")], [v("orep")])
+    act(v("s1"), bank(5, 0, C), AF.Copy)
+    fill(v("tt", 320, 512), 0.0)
+    affine([(BH, H_, BIG, 0.0), (BN, H_, -BIG, BIG), (pf(36, 4), v("me", 0, 4), BIG / 4, 0.0),
+            (pf(40, 4), v("me", 0, 4), -BIG / 4, BIG), (S1K, H_, -1.0 / ZM, 0.0), (B1K, H_, -4.0, 1.0),
+            (S3K, H_, -1.0, 1.0), (B3K, H_, 1.0 - ZB, ZB), (TH1, H_, -7.0, 8.0)])
+    for j, c in enumerate([BH, MB[1], BN, MB[3]]):
+        fill(four("hi", j), c)
     tt(v("g400", 0, NT), v("orep"), v("me", 0, NT), OP.mult, off=v("so16", 0, 5))
     scan(v("pp", 0, NT), v("k4", 0, NT), v("g400", 0, NT))
     ts(v("w16"), pj(0), T_, OP.add)
 
-    def make_t(t):
-        s, f = (Z[0], 1.0) if t == 0 else (v("x32"), 2.0 ** -5)
+    def make_t(t, between=None):
+        s, f = (z(0), 1.0) if t == 0 else (v("x32"), 2.0 ** -5)
         act(v("tt", 160, 320), s, AF.Copy, scale=f, off=v("w16", 10, 20))
         ts(v("tt", 0, 160), s, f, OP.mult, off=v("w16", 0, 10))
+        if between:
+            between()
         quant(v("qt%d" % t), v("st%d" % t), v("tt"))
         a, b = v("qt%d" % t, 0, NT), v("st%d" % t, 0, NT)
         send(u8(v("qx%d" % t, C, C + NT)), u8(a), [a], nxt, "ar%d" % t)
         send(ap(v("sx%d" % t, C, C + NT)), ap(b), [b], nxt, "ar%d" % t)
 
     def held_table(t, k0, k1, first, kh):
-        act(U0, k0, AF.Abs, bias=NKQ)
-        act(U1, k1, AF.Abs, bias=NKQ)
+        act(U0, k0, AF.Abs, scale=-1.0, bias=KQ)
+        act(U1, k1, AF.Abs, scale=-1.0, bias=KQ)
         act(first, U0, AF.Relu, scale=-40.0 * (2 * t + 1), bias=40.0 * (2 * t + 1))
         for j in (0, 2):
             act(kk(kh, j), U1, AF.Relu, scale=-40.0 * (2 * t + 2), bias=40.0 * (2 * t + 2))
 
-    def thresholds():
+    def places(p):
+        affine([(four("ko", 1), p, S1K, B1K), (four("ko", 3), p, S3K, B3K)])
+
+    def waits_for(d, js):
+        affine([(four("hi", j), d, MS[j], [BH, MB[1], BN, MB[3]][j]) for j in js])
+
+    def steps(k, code):
+        for j in (1, 2, 3):
+            ts(aa(k, j), code, TH[4 - j], OP.is_ge)
+
+    def limits():
+        tt(v("th"), v("bg", 0, C, 4), v("hi"), OP.subtract)
+
+    def flight0():
         act(v("bg"), v("s1"), AF.Copy, off=v("b16"))
+        act(kk(KC1, 3), pj(0), bias=T_)
+        tt(v("g400", NT, 400), v("orep"), v("me", NT, 400), OP.mult, off=v("so16", 6, 26))
+        act(v("k4", NT, 400), v("n4", NT, 400), AF.Sign)
+        act(v("xph"), z(0), AF.Copy, scale=0.5, off=v("w16"))
+        for b in range(4):
+            a = 528 * (b % 2) + 2 - 2 * (b // 2)
+            quant(v("qe", 128 * b, 128 * b + 128), v("se", 128 * b, 128 * b + 128), v("et", a, a + 512))
+        limits()
+        scan(v("pp", NT, 400), v("k4", NT, 400), v("g400", NT, 400))
+        quant(v("qv"), v("sv"), v("vt"))
+        tt(v("dp"), v("pp", NT + 3, 400, 4), v("pp", 3, C, 4), OP.subtract)
+        places(kk(KC1, 3))
+        affine([(four("ko", 2), four("hi", 0), 1.25 / BIG, -0.25), (four("kc", 2), four("hi", 0), -8.0 / BIG, 8.0),
+                (four("kc", 3), four("hi", 0), 1.0 / BIG, 1.0), (CM, H_, -ZM - 2.0, 2.0), (CA, H_, ZB + 2.0, -ZB - 1.75),
+                (pf(32, 3), v("c320", 1, 4), TH1, 0.0), (NI, I_, -1.0, 1.0)])
+        whole(v("tab", 0, 40), -1)
+        iota(v("tab", 40, 280), [[80, 3], [1, 2], [2, 40]])
+        for k, j in ((KK0, 0), (KK1, 0), (KK1, 2)):
+            whole(kk(k, j), 1)
 
     def flight(t):
-        if t == 0:
-            ts(v("b16"), pj(0), 0.25, OP.mult)
-            thresholds()
-            act(v("xph"), Z[0], AF.Copy, scale=0.5, off=v("w16"))
-            quant(v("qe"), v("se"), v("et"))
-            tt(DL, pj(0), DUMP, OP.subtract)
-            ms(v("kk", NT * KH1 + 3, NT * KOFF + NT, 4), 0.0)
-            cp(kk(KOFF, 2), DUMP)
-            ts(kk(KOFF, 0), DL, I_, OP.mult)
-            ts(kk(KOFF, 1), DL, NI, OP.mult)
-            tt(v("th"), v("bg", 0, C, 4), v("mt"), OP.max)
-            tt(v("g400", NT, 400), v("orep"), v("me", NT, 400), OP.mult, off=v("so16", 6, 26))
-            ms(v("kk", NT * KC1 + 2, NT * KK0 + NT, 4), 0.0)
-            scan(v("pp", NT, 400), v("k4", NT, 400), v("g400", NT, 400))
-            ms(v("kk", NT * KX1 + 1, NT * KK1 + NT, 4), 0.0)
-            tt(v("dp"), v("pp", NT + 3, 400, 4), v("pp", 3, C, 4), OP.subtract)
-            act(BASE1, DUMP, bias=-960.0)
-            act(BASE2, DUMP, bias=-640.0)
-            fill(v("tab", 0, 40), -1.0)
-            act(kk(KH0, 3), v("m16"), scale=0.125, bias=H_)
-            act(NKQ, KQ, scale=-1.0)
-            act(SD, I_, scale=312.0, bias=-316.0)
-            act(NEG, I_, scale=-1.0)
-            ts(C0, KQ, 0.0, OP.is_equal, 40.0, OP.mult)
-            ts(C1, KQ, 1.0, OP.is_equal, 80.0, OP.mult)
-            quant(v("qv"), v("sv"), v("vt"))
-            acp(kk(KW1, 0), dpj(1))
-            act(kk(KW1, 1), dpj(0), scale=NI)
-            act(kk(KW1, 2), dpj(0), scale=I_)
-            acp(kk(KW1, 3), pj(0))
-            for k, col in ((KC1, [dpj(1), dpj(0), None, pj(0)]), (KX1, [dpj(2), None, dpj(1), pj(1)]),
-                           (KX2, [dpj(3), None, dpj(2), pj(2)]), (KC3, [dpj(3), dpj(2), None, pj(2)])):
-                for j, s in enumerate(col):
-                    if s is not None:
-                        acp(kk(k, j), s)
-            return
-        oc_ = OC1 if t == 1 else OC2
-        if t == 2:
-            scan(oo(OK0), aa(1), kk(KK0))
-            scan(oo(OK1), aa(1), kk(KK1))
+        oc_, ow = (OC1, OW1) if t == 1 else (OC2, OW2)
+        act(z(t, 2, 1280, 4), v("x32", 2, 1280, 4), AF.Copy, scale=2.0 ** -5)
+        cp(v("x16"), oo(oc_, 3))
+        ts(z(t, 3, 1280, 4), v("x32", 3, 1280, 4), 2.0 ** -5, OP.mult)
+        scan(oo(ow), aa(t), kk(KW1 if t == 1 else KW2))
         act(v("xph"), v("x32"), AF.Copy, scale=2.0 ** -6, off=v("x16"))
-        if t == 2:
-            held_table(2, oo(OK0, 3), oo(OK1, 3), W0_, KH2)
-        for b in (2, 3):
-            ts(v("z%d" % t, b, 1280, 4), v("x32", b, 1280, 4), 2.0 ** -5, OP.mult)
-        tt(DL, oo(oc_, 3), DUMP, OP.subtract)
-        quant(QX[t][0], QX[t][1], Z[t])
-        mm(bank(5, 0, C), UR[0], UR[1], QX[t][0], QX[t][1])
+        for k in range(2):
+            a, b = hc * k, hc * k + hc
+            quant(v("qx%d" % t, a, b), v("sx%d" % t, a, b), z(t, 4 * a, 4 * b))
+            mm(bank(5 + k, 0, hc), UR[0], UR[1], v("qx%d" % t, a, b), v("sx%d" % t, a, b))
+        ts(v("b16"), oo(ow, 3), T_, OP.subtract, 0.25, OP.mult)
         if t == 1:
-            for k, j, c in ((KK0, 0, 1.0), (KK1, 0, 1.0), (KK1, 2, 1.0), (KH0, 0, C1), (KH0, 2, C1)):
-                fill(kk(k, j), c)
-        act(v("s1"), bank(5, 0, C), AF.Copy)
-        thresholds()
-        if t == 1:
-            tt(F_, aa(0, 3), aa(0, 2), OP.subtract)
-            tt(K01, aa(0, 2), aa(0, 1), OP.add)
-            tt(TA, aa(0, 3), aa(0, 1), OP.add)
-            ts(TD, F_, SC_, OP.mult, T_, OP.add)
-            ts(E2_, F_, I_, OP.mult, NI, OP.add)
-            ts(K11, TA, 1.0, OP.add)
-            tt(TD, TD, BASE1, OP.add)
-            tt(kk(KOFF, 1), E2_, DL, OP.mult)
-            scan(oo(OX1N), aa(3), kk(KX1))
-            cp(v("s16"), TD)
-            tt(kk(KOFF, 0), DL, kk(KOFF, 1), OP.subtract)
-            scan(oo(OX2N), aa(3), kk(KX2))
-            scan(oo(OX1), aa(0), kk(KX1))
-            scan(oo(OX2), aa(0), kk(KX2))
-            scan(oo(OC3), aa(0), kk(KC3))
-            tt(DN, oo(OX1N, 3), oo(OWN, 3), OP.subtract)
-            tt(kk(KW2N, 0), oo(OX2N, 3), oo(OX1N, 3), OP.subtract)
-            tt(DO, oo(OX1, 3), oo(OW1, 3), OP.subtract)
-            tt(kk(KW2, 0), oo(OX2, 3), oo(OX1, 3), OP.subtract)
-            tt(kk(KC2, 0), oo(OC3, 3), oo(OX1, 3), OP.subtract)
-            tt(kk(KC2, 1), oo(OX1, 3), oo(OC1, 3), OP.subtract)
-            tt(kk(KK0, 1), K11, K01, OP.subtract)
-            tt(v("th"), v("bg", 0, C, 4), v("mt"), OP.max)
-            held_table(1, K01, K11, V0_, KH1)
+            tt(F_, aa(A0, 3), aa(A0, 2), OP.subtract)
+            scan(oo(OX1N), aa(AN0), kk(KX1))
+            scan(oo(OX1), aa(A0), kk(KX1))
+            d, js = D1, (1, 3)
         else:
-            scan(oo(OE2), aa(1), kk(KE2))
-            tt(E0_, FN, aa(1, 1), OP.mult)
-            tt(kk(KS2, 3), FA, BASE2, OP.add)
-            tt(TE, oo(OE2, 3), DL, OP.mult)
-            tt(TD, E0_, DL, OP.mult)
-            scan(oo(OS2), aa(1), kk(KS2))
-            tt(kk(KOFF, 0), DL, TE, OP.subtract)
-            tt(kk(KOFF, 2), TD, DUMP, OP.add)
-            tt(kk(KOFF, 1), TE, TD, OP.subtract)
-            ts(v("s16"), oo(OS2, 3), T_, OP.add)
-            tt(kk(KH2, 1), W0_, kk(KH2, 0), OP.subtract)
+            scan(oo(OD2), aa(A1), kk(KD2))
+            scan(oo(OK0), aa(A1), kk(KK0))
+            scan(oo(OK1), aa(A1), kk(KK1))
+            d, js = oo(OD2, 3), (0, 1, 2, 3)
+        act(v("s1", 0, hc), bank(5, 0, hc), AF.Copy)
+        cp(v("s1", hc, C), bank(6, 0, hc))
+        if t == 1:
+            act(D1, F_, scale=SB)
+            scan(oo(OX2N), aa(AN0), kk(KX2))
+        else:
+            tt(TD, LB, d, OP.subtract)
+        act(v("bg", hc, C), v("s1"), AF.Copy, off=v("b16", 10, 20))
+        cp(v("bg", 0, hc), v("s1"), off=v("b16", 0, 10))
+        waits_for(d, js)
+        places(oo(oc_, 3))
+        if t == 1:
+            tt(TD, LB, d, OP.subtract)
+            scan(oo(OX2), aa(A0), kk(KX2))
+        else:
             tt(kk(KH1, 1), V0_, kk(KH1, 0), OP.subtract)
-            scan(v("oo", NT * OH0, NT * OH1 + NT), v("aa", 0, 2 * NT), v("kk", NT * KH0, NT * KH1 + NT))
-            tt(kk(KH2, 3), oo(OH0, 3), oo(OH1, 3), OP.add)
-            tt(v("th"), v("bg", 0, C, 4), v("mt"), OP.max)
+            scan(oo(OH0), aa(A0), kk(KH0))
+        ts(v("s16"), TD, float(C * t), OP.add)
+        limits()
 
-    make_t(0)
+    make_t(0, lambda: ts(v("b16"), pj(0), 0.25, OP.mult))
+    flight0()
     for t in range(R):
-        flight(t)
+        last = t == R - 1
         arrive([v("qx%d" % t, C, C + NT), v("sx%d" % t, C, C + NT)], "ar%d" % t, 2 * prv[4])
         mq, msc = v("qx%d" % t, 272, 400), v("sx%d" % t, 272, 400)
         mm(bank(4, 0, 128), UR[0], UR[1], mq, msc)
@@ -441,92 +458,137 @@ def build(T, nxt, prv):
 
         if t:
             keep()
-        tt(v("acc"), bank(4, 48, 128), v("th"), OP.is_ge)
-        scan(v("cd"), v("kc"), v("acc"))
         code = v("cd", 3, NT, 4)
-        if t < R - 1:
-            cp(v("ls%d" % t, 0, 20), code)
-            send(ap(v("lr%d" % t, 0, 20)), ap(v("ls%d" % t, 0, 20)), [v("ls%d" % t, 0, 20)], prv, "li%d" % t)
-        ts(aa(t, 1), code, 3.0, OP.is_ge)
-        ts(aa(t, 2), code, 2.0, OP.is_ge)
-        scan(oo(OOFF), aa(t), kk(KOFF))
+        lst = v("ls%d" % min(t, 1), 0, 20)
+        tt(v("acc", NT, 2 * NT), bank(4, 48, 128), v("th"), OP.is_ge)
+        tt(v("acc", 0, NT), bank(4, 48, 128), v("bg", 0, C, 4), OP.is_ge)
+        scan(v("cd", NT, 2 * NT), v("ko"), v("acc", NT, 2 * NT))
+        scan(v("cd", 0, NT), v("kc"), v("acc", 0, NT))
+        ts(v("o16"), v("cd", NT + 3, 2 * NT, 4), CM, OP.mult, CA, OP.add)
+        if t == 0:
+            acp(lst, code)
+        if t == 1:
+            cp(lst, code)
+        if not last:
+            send(ap(v("lr%d" % t, 0, 20)), ap(lst), [lst], prv, "li%d" % t)
         if t == 0:
             for b in range(4):
                 tt(v("bl", b, C, 4), bank(b, 48, 128), v("xph", b, C, 4), OP.add)
-                if b == 0:
-                    ts(v("o16"), oo(OOFF, 2), T_, OP.add)
+            acp(kk(KW1, 0), dpj(1))
+            affine([(kk(KW1, 1), dpj(0), NI, 0.0), (kk(KW1, 2), dpj(0), I_, 0.0)])
+            acp(kk(KW1, 3), kk(KC1, 3))
             keep()
-            act(CDF, C1, scale=-1.0, bias=C0)
-            fill(kk(KH0, 1), CDF)
+            for k, j, s in ((KC1, 0, 1), (KC1, 1, 0), (KX1, 0, 2), (KX1, 2, 1), (KX2, 0, 3), (KX2, 2, 2), (KC3, 0, 3), (KC3, 1, 2)):
+                acp(kk(k, j), dpj(s))
+            for k, s in ((KX1, 1), (KX2, 2), (KC3, 2)):
+                act(kk(k, 3), pj(s), bias=T_)
+            affine([(SB, I_, 320.0, 0.0), (LB, v("m16"), 1.0, Q_)])
         else:
-            ts(v("o16"), oo(OOFF, 2), T_, OP.add)
+            if t == 1:
+                tt(ln(8, 2), oo(OX1N, 3, 2), oo(OWN, 3, 2), OP.subtract)
+                tt(kk(KW2N, 0, 2), oo(OX2N, 3, 2), oo(OX1N, 3, 2), OP.subtract)
             tt(v("bl"), v("kept", 0, C * t + C), v("xph"), OP.add, off=v("s16"))
         if t == 1:
-            for kn, d, w in ((KW2, DO, oo(OW1, 3)), (KW2N, DN, oo(OWN, 3))):
-                act(kk(kn, 1), d, scale=NI)
-                act(kk(kn, 2), d, scale=I_)
-                acp(kk(kn, 3), w)
+            affine([(kk(KW2N, 1, 2), ln(8, 2), NI, 0.0), (kk(KW2N, 2, 2), ln(8, 2), I_, 0.0)])
+            acp(kk(KW2N, 3, 2), oo(OWN, 3, 2))
             acp(kk(KC2, 3), oo(OC1, 3))
-            act(kk(KE2, 0), F_, scale=I_)
-            act(kk(KE2, 1), F_, scale=0.0, bias=NEG)
-            act(kk(KE2, 2), F_, scale=NEG, bias=I_)
-            acp(kk(KE2, 3), E2_)
-            acp(kk(KK0, 3), K01)
-            acp(kk(KK1, 3), K11)
-            act(kk(KS2, 0), F_, scale=SD)
-            act(kk(KS2, 1), F_, scale=SB, bias=SB)
-            act(kk(KS2, 2), F_, scale=SB, bias=SC_)
-        win = v("z%d" % t)
+            affine([(SC_, I_, -320.0, 0.0), (SD, I_, -312.0, 316.0), (kk(KD2, 1), D1, -1.0, SC_), (kk(KD2, 0), F_, SD, 0.0),
+                    (kk(KD2, 2), D1, -1.0, SB), (kk(KD2, 3), D1, 2.0, 0.0), (kk(KK0, 1), F_, 1.0, 1.0), (CDF, C1, -1.0, C0)])
+            for j, c in ((0, C1), (2, C1), (1, CDF)):
+                fill(kk(KH0, j), c)
+            act(kk(KH0, 3), v("m16"), scale=0.125, bias=H_)
+        if t == 2:
+            acp(kk(KH1, 3), oo(OH0, 3))
+            held_table(2, oo(OK0, 3), oo(OK1, 3), W0_, KH2)
+        win = z(t, 0, ZW)
         add("V", lambda q, win=win: q.tensor_copy(ap(win).indirect(ap(v("o16"))), ap(v("bl"))), [v("o16"), v("bl")], [win])
-        quant(v("qz"), v("sz"), Z[t])
-        for b in range(4):
-            act(v("z32", C * b, C * b + C), v("z%d" % t, b, 1280, 4), AF.Copy, scale=32.0)
-        for b in range(4):
-            mm(bank(b, 0, C), v("qw", 128 * b, 128 * b + 128), v("sw", 128 * b, 128 * b + 128), v("qz"), v("sz"))
-        ts(aa(t, 3), code, 1.0, OP.is_ge)
-        if t == R - 1:
-            scan(oo(OH), aa(2), kk(KH2))
-            cp(v("h16"), oo(OH, 3))
-        else:
-            kw, ow, kc_, oc_ = (KW1, OW1, KC1, OC1) if t == 0 else (KW2, OW2, KC2, OC2)
-            scan(oo(oc_), aa(t), kk(kc_))
-            scan(oo(ow), aa(t), kk(kw))
-            ts(v("x16"), oo(oc_, 3), T_, OP.add)
-            ts(v("b16"), oo(ow, 3), 0.25, OP.mult)
-            arrive([v("lr%d" % t, 0, 20)], "li%d" % t, nxt[4])
-        on, kn = (OWN, KW1) if t == 0 else (OWN2, KW2N)
-        for b in range(4):
-            if b == 2 and t < R - 1:
-                for j in range(1, 4):
-                    ts(aa(3 + t, j), v("lr%d" % t, 0, 20), float(4 - j), OP.is_ge)
-            if b == 3 and t < R - 1:
-                scan(oo(on), aa(3 + t), kk(kn))
-            tt(v("x32", b, 1280, 4), bank(b, 0, C), v("z32", C * b, C * b + C), OP.add)
-            if b < 2:
-                act(v("z%d" % (t + 1), b, 1280, 4), v("x32", b, 1280, 4), AF.Copy, scale=2.0 ** -5)
-        if t < R - 1:
-            ts(v("w16"), oo(on, 3), T_, OP.add)
-            make_t(t + 1)
-        if t == 1:
-            act(FA, F_, scale=SA)
-            act(FN, F_, scale=NI)
 
-    for b in (2, 3):
-        ts(v("z3", b, 1280, 4), v("x32", b, 1280, 4), 2.0 ** -5, OP.mult)
-    for k in range(2):
-        a, b = hc * k, hc * k + hc
-        quant(v("qx3", a, b), v("sx3", a, b), v("z3", 4 * a, 4 * b))
-        mm(bank(4 + k, 0, hc), v("qv"), v("sv"), v("qx3", a, b), v("sx3", a, b))
-    act(v("skr"), v("tab"), AF.Copy, off=v("h16"))
-    dma("S", T.oc[:, :], u8(v("qx3")), [v("qx3")], [], "o0")
-    for k in range(2):
-        cp(v("yb", hc * k, hc * k + hc), bank(4 + k, 0, hc))
-    dma("A", T.sk[:, :], T.skr[0:128:16, :], [v("skr")], [], "o1")
-    for k in range(2):
-        r = v("yb", hc * k, hc * k + hc)
-        dma("S", T.y[:, hc * k:hc * k + hc], ap(r), [r], [], "o%d" % (6 + k))
-    for k in range(4):
-        dma("A", T.osc[4 * k:4 * k + 4, :], T.sx3[32 * k:32 * k + 4, :], [v("sx3")], [], "o%d" % (2 + k))
+        def layer(b, a, e, k):
+            mm(bank(k, 0, e - a), v("qw", 128 * b, 128 * b + 128), v("sw", 128 * b, 128 * b + 128), v("qz", a, e), v("sz", a, e))
+
+        def plus(b, a, e, k):
+            tt(v("x32", 4 * a + b, 4 * e, 4), bank(k, 0, e - a), v("z32", C * b + a, C * b + e), OP.add)
+
+        def back32(b):
+            act(z(t + 1, b, 1280, 4), v("x32", b, 1280, 4), AF.Copy, scale=2.0 ** -5)
+
+        parts = [(0, 0, hc, 6), (0, hc, C, 7), (1, hc, C, 1), (2, 0, C, 2), (3, 0, hc, 3), (3, hc, C, 0), (1, 0, hc, 4)]
+        for k in range(2):
+            quant(v("qz", hc * k, hc * k + hc), v("sz", hc * k, hc * k + hc), z(t, 4 * hc * k, 4 * hc * (k + 1)))
+        for b in range(4):
+            act(v("z32", C * b, C * b + C), z(t, b, 1280, 4), AF.Copy, scale=32.0)
+        for k in (0, 6, 1, 2, 3, 4, 5):
+            layer(*parts[k])
+        steps(A0 + t, code)
+        plus(*parts[0])
+        plus(*parts[6])
+        plus(*parts[1])
+        back32(0)
+        if not last:
+            an, on, kn = (AN0, OWN, KW1) if t == 0 else (AN1, OWN2, KW2N)
+            if t == 1:
+                scan(oo(OC3), aa(A0), kk(KC3))
+                tt(kk(KC2, 1), oo(OX1, 3), oo(OC1, 3), OP.subtract)
+            plus(*parts[2])
+            back32(1)
+            arrive([v("lr%d" % t, 0, 20)], "li%d" % t, nxt[4])
+            steps(an, v("lr%d" % t, 0, 20))
+            plus(*parts[3])
+            scan(oo(on), aa(an), kk(kn))
+            if t == 1:
+                tt(kk(KC2, 0), oo(OC3, 3), oo(OX1, 3), OP.subtract)
+            plus(*parts[4])
+            cp(v("w16"), oo(on, 3))
+            plus(*parts[5])
+            make_t(t + 1, lambda: scan(oo(OC1 if t == 0 else OC2), aa(A0 + t), kk(KC1 if t == 0 else KC2)))
+            flight(t + 1)
+            if t == 0:
+                tt(K01, aa(A0, 2), aa(A0, 1), OP.add)
+                tt(TA, aa(A0, 3), aa(A0, 1), OP.add)
+                act(K11, TA, bias=1.0)
+                acp(kk(KK0, 3), K01)
+                act(kk(KK1, 3), TA, bias=1.0)
+                held_table(1, K01, K11, V0_, KH1)
+            continue
+
+        scan(oo(OH1), aa(A1), kk(KH1))
+        tt(kk(KH2, 1), W0_, kk(KH2, 0), OP.subtract)
+        plus(*parts[2])
+        back32(1)
+        cp(kk(KH2, 3), oo(OH1, 3))
+        plus(*parts[3])
+        scan(oo(OH), aa(A2), kk(KH2))
+        plus(*parts[4])
+        cp(v("h16"), oo(OH, 3))
+        act(v("skr"), v("tab"), AF.Copy, off=v("h16"))
+        dma("A", T.sk[:, :], T.skr[0:128:16, :], [v("skr")], [], "o8")
+
+        def back(b, k):
+            a, e = 4 * hc * k + b, 4 * hc * (k + 1)
+            ts(z(3, a, e, 4), v("x32", a, e, 4), 2.0 ** -5, OP.mult)
+
+        def finish(k):
+            a, e = hc * k, hc * k + hc
+            quant(v("qx3", a, e), v("sx3", a, e), z(3, 4 * a, 4 * e))
+            mm(bank(4 + k, 0, hc), v("qv"), v("sv"), v("qx3", a, e), v("sx3", a, e))
+            dma("S", T.oc[:, 4 * a:4 * e], u8(v("qx3", a, e)), [v("qx3", a, e)], [], "o%d" % k)
+
+        def result(k):
+            r = v("yb", hc * k, hc * k + hc)
+            cp(r, bank(4 + k, 0, hc))
+            dma("S", T.y[:, hc * k:hc * k + hc], ap(r), [r], [], "o%d" % (6 + k))
+
+        back(2, 0)
+        back(3, 0)
+        plus(*parts[5])
+        back(2, 1)
+        finish(0)
+        back(3, 1)
+        finish(1)
+        for k in range(4):
+            dma("A", T.osc[4 * k:4 * k + 4, :], T.sx3[32 * k:32 * k + 4, :], [v("sx3")], [], "o%d" % (2 + k))
+        result(0)
+        result(1)
     return ops
 
 

from concourse.mybir import dt, AluOpType, ActivationFunctionType

C, NT, R = 320, 80, 3
H = float(2.0 ** 90)
BIG = float(2.0 ** 80)
F32, BF, I32, U16, CODE, PL = "float32", "bfloat16", "int32", "uint16", "float8_e4m3fn_x4", "uint8"
ACT_ROWS = [19, 18, 17]
TILE_AT = {4: 0, 3: 320, 2: 576, 1: 832, 0: 960}
TILE_W = {4: 320, 3: 256, 2: 256, 1: 128, 0: 128}
ZW, ZB, ZM = 10240, 7680.0, 1280.0


def _sb(n, d):
    return ("sbuf", [128, n], d)


SCRATCH = {
    "ps": ("psum", [128, 4096], F32),
    "ut": _sb(512, BF), "vt": _sb(512, BF), "qu": _sb(128, CODE), "su": _sb(128, PL), "qp": _sb(256, CODE), "sp": _sb(256, PL),
    "qv": _sb(128, CODE), "sv": _sb(128, PL), "qw": _sb(512, CODE), "sw": _sb(512, PL),
    "gt": _sb(512, BF), "qg": _sb(128, CODE), "sg": _sb(128, PL),
    "et": _sb(1056, BF), "qe": _sb(512, CODE), "se": _sb(512, PL), "zero": _sb(528, BF),
    "cmp": _sb(4 * 1088, BF), "qc": _sb(1088, CODE), "scm": _sb(1088, PL), "sig": _sb(4 * C, BF), "junk": _sb(2304, BF),
    "zz": _sb(3 * 1280 + ZW, BF),
    "x32": _sb(1280, BF), "z32": _sb(1280, BF), "qz": _sb(C, CODE), "sz": _sb(C, PL),
    "qx0": _sb(400, CODE), "sx0": _sb(400, PL), "qx1": _sb(400, CODE), "sx1": _sb(400, PL),
    "qx2": _sb(400, CODE), "sx2": _sb(400, PL), "qx3": _sb(C, CODE), "sx3": _sb(C, PL),
    "tt": _sb(512, BF), "qt0": _sb(128, CODE), "st0": _sb(128, PL), "qt1": _sb(128, CODE), "st1": _sb(128, PL),
    "qt2": _sb(128, CODE), "st2": _sb(128, PL),
    "kept": _sb(960, BF), "xph": _sb(C, F32), "bl": _sb(C, BF),
    "pi": _sb(16, I32), "pf": _sb(64, F32),
    "uo": _sb(16, F32), "uo16": _sb(16, U16), "so": _sb(26, F32), "so16": _sb(26, U16), "q16": _sb(20, U16),
    "nm": _sb(32, BF), "blk": _sb(512, BF), "n4": _sb(400, BF), "c320": _sb(C, F32), "m16": _sb(20, F32),
    "p16": _sb(96, BF), "mm": _sb(C, BF), "k320": _sb(C, BF), "kr": _sb(C, BF), "kb": _sb(C, BF), "dsc": _sb(C, BF),
    "me": _sb(400, BF), "k4": _sb(400, BF), "kc": _sb(NT, F32), "hi": _sb(NT, F32), "ko": _sb(NT, F32),
    "vv": _sb(C, F32), "sc": _sb(C, F32), "rs": _sb(C, F32), "rk16": _sb(20, U16), "orep": _sb(C, F32),
    "miss": _sb(60, F32),
    "g400": _sb(400, F32), "pp": _sb(400, F32), "dp": _sb(NT, F32),
    "s1": _sb(C, F32), "bg": _sb(C, F32), "th": _sb(NT, F32), "acc": _sb(2 * NT, F32), "cd": _sb(2 * NT, F32),
    "aa": _sb(5 * NT, F32), "kk": _sb(14 * NT, F32), "oo": _sb(18 * NT, F32), "ln": _sb(20 * 20, F32),
    "w16": _sb(20, U16), "b16": _sb(20, U16), "x16": _sb(20, U16), "s16": _sb(20, U16), "o16": _sb(20, U16), "h16": _sb(20, U16),
    "ls0": _sb(24, BF), "ls1": _sb(24, BF), "lr0": _sb(24, BF), "lr1": _sb(24, BF),
    "tab": _sb(280, F32), "skr": _sb(C, F32), "yb": _sb(C, F32),
}
SEMAPHORES = ["sv_", "sa_", "sp_", "sg_", "dx0", "dx1", "du", "dwc", "dws", "dv", "ar0", "ar1", "ar2", "li0", "li1", "loc",
              "o0", "o1", "o2", "o3", "o4", "o5", "o6", "o7", "o8"]
ENG_SEM = {"V": "sv_", "A": "sa_", "P": "sp_", "G": "sg_"}


def build(T, nxt, prv):
    ops = []
    OP = AluOpType
    AF = ActivationFunctionType

    def v(name, a=0, b=None, s=1):
        return (name, a, SCRATCH[name][1][1] if b is None else b, s)

    def ap(r):
        return T[r[0]][:, r[1]:r[2]:r[3]] if r[3] != 1 else T[r[0]][:, r[1]:r[2]]

    def bank(k, a, b):
        return v("ps", 512 * k + a, 512 * k + b)

    def add(eng, fn, rd, wr, sem=None, cnt=0, acc=False, kind="op"):
        ops.append({"e": eng, "fn": fn, "rd": [r for r in rd if isinstance(r, tuple)], "wr": wr, "sem": sem, "cnt": cnt,
                    "acc": acc, "kind": kind})

    def sx(x):
        return ap(x) if isinstance(x, tuple) else x

    def src(x, off):
        return ap(x) if off is None else ap(x).indirect(ap(off))

    def ts(out, in0, s1, op0, s2=None, op1=None, off=None):
        if op1 is None:
            add("V", lambda q: q.tensor_scalar(ap(out), src(in0, off), sx(s1), None, op0), [in0, s1, off], [out])
        else:
            add("V", lambda q: q.tensor_scalar(ap(out), src(in0, off), sx(s1), sx(s2), op0, op1), [in0, s1, s2, off], [out])

    def tt(out, in0, in1, op, off=None):
        add("V", lambda q: q.tensor_tensor(ap(out), src(in0, off), ap(in1), op), [in0, in1, off], [out])

    def cp(out, in_, off=None):
        add("V", lambda q: q.tensor_copy(ap(out), src(in_, off)), [in_, off], [out])

    def ms(out, c):
        add("V", lambda q: q.memset(ap(out), c), [], [out])

    def scan(out, d0, d1, op0=OP.mult, op1=OP.add, init=0.0):
        add("V", lambda q: q.tensor_tensor_scan(ap(out), ap(d0), ap(d1), init, op0, op1), [d0, d1], [out])

    def quant(qc, qs, in_):
        add("V", lambda q: q.quantize_mx(ap(qc), ap(qs), ap(in_)), [in_], [qc, qs])

    def act(out, in_, func=AF.Identity, scale=None, bias=None, off=None, total=None):
        kw = {}
        if scale is not None:
            kw["scale"] = sx(scale)
        if bias is not None:
            kw["bias"] = sx(bias)
        if total is not None:
            kw["accum_out"] = ap(total)
        add("A", lambda q: q.activation(ap(out), src(in_, off), func, **kw), [in_, scale, bias, off],
            [out] if total is None else [out, total])

    def acp(out, in_):
        act(out, in_, AF.Copy)

    def fill(out, c):
        act(out, v("k320", 0, len(range(out[1], out[2], out[3]))), scale=0.0, bias=c)

    def affine(rows):
        for o, i_, s, b in rows:
            act(o, i_, scale=s, bias=b)

    def mm(out, lq, ls, rq, rs_, start=True, stop=True):
        add("P", lambda q: q.matmul_mx(ap(out), ap(lq), ap(ls), ap(rq), ap(rs_), start, stop), [lq, ls, rq, rs_], [out],
            acc=not start)

    def iota(out, pattern, base=0, ch=0):
        if SCRATCH[out[0]][2] == I32:
            add("G", lambda q: q.iota(ap(out), pattern, base, ch), [], [out])
        else:
            add("G", lambda q: q.iota(ap(out), pattern, base, ch, allow_small_or_imprecise_dtypes=True), [], [out])

    def whole(out, c):
        iota(out, [[0, len(range(out[1], out[2], out[3]))]], c)

    def dma(eng, out, in_, rd, wr, sem):
        add(eng, lambda q: q.dma_start(out, in_), rd, wr, sem=sem, cnt=16, kind="dma")

    def send(out, in_, rd, to, sem):
        add("G", lambda q: q.remote_dma(out, in_, T.sem[sem], T.sem["loc"], to[1], to[0], to[2]), rd, [], kind="send", cnt=to[3])

    def arrive(wr, sem, cnt):
        add("X", None, [], wr, sem=sem, cnt=cnt, kind="arrive")

    def u8(r):
        return ap(r).bitcast(dt.uint8)

    def u32(r):
        return ap(r).bitcast(dt.uint32)

    def pick(to, off):
        add("V", lambda q: q.tensor_copy(u32(to[0]), u32(v("qu")).indirect(ap(off))), [v("qu"), off], [to[0]])
        add("A", lambda q: q.activation(ap(to[1]), ap(v("su")).indirect(ap(off)), AF.Copy), [v("su"), off], [to[1]])

    def pf(k, n=1):
        return v("pf", k, k + n)

    def ln(k, n=1):
        return v("ln", 20 * k, 20 * (k + n))

    def kk(k, j=None, n=1):
        return v("kk", NT * k + (j or 0), NT * (k + n), 1 if j is None else 4)

    def oo(k, j=None, n=1):
        return v("oo", NT * k + (j or 0), NT * (k + n), 1 if j is None else 4)

    def aa(k, j=None, n=1):
        return v("aa", NT * k + (j or 0), NT * (k + n), 1 if j is None else 4)

    def four(name, j):
        return v(name, j, NT, 4)

    def pj(j):
        return v("pp", NT * j + 3, NT * j + NT, 4)

    def dpj(j):
        return v("dp", 20 * j, 20 * j + 20)

    def z(t, a=0, b=1280, s=1):
        return v("zz", 1280 * (3 - t) + a, 1280 * (3 - t) + b, s)

    Q_, GP, T_, I_, H_, HB = [pf(k) for k in range(1, 7)]
    (QQ, KQ, Q1, SO, NI, RS, SB, SC_, SD, IRS, IR0, CQ, C0, C1, CDF, S1K, B1K, S3K, B3K, CM, CA, BH, BN,
     TH1) = [pf(k) for k in range(8, 32)]
    TH = {c: pf(31 + c) for c in (1, 2, 3)}
    MS, MB = [pf(36 + j) for j in range(4)], [pf(40 + j) for j in range(4)]
    YY, YI, F_, TA, TD, XX, D1, LB, DN, DO, K01, K11, U0, U1, V0_, W0_ = [ln(k) for k in range(16)]
    KC1, KC3, KC2, KK0, KX1, KX2, KK1, KH0, KH1, KH2, KW1, KW2N, KW2, KD2 = range(14)
    OWN, OW1, OX1N, OX1, OX2N, OX2, OC1, OC3, OW2, OC2, OD2, OH, OWN2, OK0, OK1, OH0, OH1 = range(17)
    AN0, A0, A1, A2, AN1 = range(5)
    QX = [(v("qx%d" % t, 0, C), v("sx%d" % t, 0, C)) for t in range(4)]
    UO = (v("qp", 0, 128), v("sp", 0, 128))
    UR = (v("qp", 128, 256), v("sp", 128, 256))
    hc = C // 2

    dma("A", ap(v("ut")), T.u[:, :], [], [v("ut")], "du")
    for k in range(2):
        dma("S", ap(z(0, 640 * k, 640 * k + 640)), T.x[:, 640 * k:640 * k + 640], [], [z(0, 640 * k, 640 * k + 640)], "dx%d" % k)
    dma("S", u8(v("qw")), T.wc[:, :], [z(0, 1272, 1280)], [v("qw")], "dwc")
    dma("S", ap(v("sw")), T.ws[:, :], [], [v("sw")], "dws")
    dma("S", ap(v("vt")), T.v[:, :], [], [v("vt")], "dv")
    iota(v("pi", 0, 1), [[0, 1]], 0, 1)
    iota(v("nm", 0, 16), [[1, 16]])
    iota(v("m16"), [[16, 20]])
    iota(v("uo"), [[1, 2], [16, 8]])
    iota(v("blk"), [[1, 8], [0, 64]])
    iota(v("n4"), [[0, 100], [1, 4]])
    iota(v("so", 0, 6), [[64, 6]])
    iota(v("so", 6, 26), [[1, 4], [64, 5]], 1)
    iota(v("c320"), [[1, C]])
    iota(v("zero"), [[0, 528]])
    for e in range(2):
        o = v("et", 528 * e, 528 * e + 514)
        add("G", lambda q, o=o, e=e: q.affine_select(ap(o), ap(v("zero", 0, 514)), [[-1, 514]], OP.not_equal, 0.5, 2 + e, 4),
            [v("zero")], [o])
    iota(v("kc"), [[0, 20], [2, 4]])
    whole(four("ko", 0), 0)
    whole(v("aa", 0, 5 * NT, 4), 0)
    whole(kk(KC1, 2, 4), 0)
    whole(kk(KX1, 1, 3), 0)
    P0 = v("pi", 0, 1)

    def bits(k, sh, an):
        if sh:
            ts(v("pi", k, k + 1), P0, sh, OP.logical_shift_right, an, OP.bitwise_and)
        else:
            ts(v("pi", k, k + 1), P0, an, OP.bitwise_and)

    def beyond(k):
        return v("cmp", 4 * (TILE_AT[k] + 64 * k + 16), 4 * (TILE_AT[k] + TILE_W[k]))

    NM, EQ, KA, MM, KR = v("nm", 0, 16), v("p16", 0, 16), v("p16", 16, 32), v("p16", 32, 48), v("p16", 64, 80)
    ms(v("k320"), H)
    bits(1, 0, 15)
    bits(2, 4, 7)
    ms(v("k320", 0, C, 16), -H)
    cp(v("pf", 1, 3), v("pi", 1, 3))
    for k in (4, 3, 1):
        fill(beyond(k), 0.0)
    for k, (sh, an) in enumerate([(0, 3), (2, 1), (3, 1), (0, 1)]):
        bits(k + 3, sh, an)
    ts(EQ, NM, Q_, OP.is_equal)
    ts(Q1, Q_, 1.0, OP.add)
    ts(v("q16"), v("m16"), 0.0, OP.mult, Q_, OP.add)
    cp(v("pf", 3, 7), v("pi", 3, 7))
    ts(MM, EQ, 2.0 * H, OP.mult, -H, OP.add)
    ts(KA, NM, Q1, OP.is_equal, 16383.0, OP.mult)
    cp(v("uo16"), v("uo"))
    ts(IR0, Q_, 15.0, OP.is_equal)
    act(v("mm"), MM, AF.Copy, off=v("q16"))
    tt(KR, KA, EQ, OP.subtract)
    ms(beyond(2), 0.0)
    ms(beyond(0), 0.0)
    ms(v("miss", 0, 1), 0.0)
    act(v("kb"), v("k320"), scale=0.5 / H, bias=0.5)
    quant(v("qu"), v("su"), v("ut"))
    pick(UO, v("uo16", 0, 8))
    act(v("kr"), KR, bias=1.0, off=v("q16"))
    affine([(IRS, IR0, -16383.0, 16384.0), (RS, IR0, 1.0 - 2.0 ** -14, 2.0 ** -14), (CQ, Q_, -1.0, 15.0),
            (QQ, H_, 2.0, I_), (KQ, H_, -8.0, Q_), (SO, HB, -0.75, Q_)])

    for k in range(2):
        a, b = hc * k, hc * k + hc
        quant(v("qx0", a, b), v("sx0", a, b), z(0, 4 * a, 4 * b))
    mm(bank(6, 0, C), UO[0], UO[1], QX[0][0], QX[0][1])
    mm(bank(7, 0, C), UO[0], UO[1], QX[0][0], QX[0][1])
    pick(UR, v("uo16", 8, 16))
    mm(bank(5, 0, C), UR[0], UR[1], QX[0][0], QX[0][1])
    ts(v("gt"), v("blk"), GP, OP.is_equal)

    def own(m):
        return v("sc", 16 * m + 15, 16 * m + 16)

    def row(m, e):
        a = 4 * TILE_AT[(m - 1) // 4]
        return v("cmp", a + (m - 1) % 4, a + 4 * e, 4)

    def miss(m):
        return v("miss", m, m + 1)

    def below(m):
        ts(row(m, 16 * m), bank(6, 0, 16 * m), own(m), OP.is_lt)
        a = 8 * m * (m - 1)
        act(v("junk", a, a + 16 * m), row(m, 16 * m), scale=IRS, total=miss(m))

    def count(k):
        a, w = TILE_AT[k], TILE_W[k]
        quant(v("qc", a, a + w), v("scm", a, a + w), v("cmp", 4 * a, 4 * (a + w)))
        if k == 4:
            mm(bank(0, 0, 192), v("qg"), v("sg"), v("qc", 128, C), v("scm", 128, C), True, False)
            a3 = TILE_AT[3] + 128
            mm(bank(0, 0, 128), v("qg"), v("sg"), v("qc", a3, a3 + 128), v("scm", a3, a3 + 128), False, False)
        if k == 2:
            mm(bank(0, 0, 128), v("qg"), v("sg"), v("qc", a + 128, a + w), v("scm", a + 128, a + w), False, True)
        mm(bank(1, 0, 128), v("qg"), v("sg"), v("qc", a, a + 128), v("scm", a, a + 128), k == 3, k == 0)

    tt(v("vv", 256, C), bank(6, 256, C), v("mm", 256, C), OP.min)
    quant(v("qg"), v("sg"), v("gt"))
    scan(v("sc", 256, C), v("k320", 256, C), v("vv", 256, C), OP.min, OP.max, -H)
    tt(v("vv", 0, 256), bank(6, 0, 256), v("mm", 0, 256), OP.min)
    nr = len(ACT_ROWS)
    for n in range(nr + 1):
        if n < nr:
            m = ACT_ROWS[n]
            act(v("sig", C * n, C * n + 16 * m), bank(7, 0, 16 * m), AF.Sign, scale=-1.0, bias=own(m))
        if n:
            m = ACT_ROWS[n - 1]
            act(row(m, 16 * m), v("sig", C * (n - 1), C * (n - 1) + 16 * m), AF.Relu, total=v("miss", 40 + m, 41 + m))
    lo = min(ACT_ROWS)
    below(16)
    act(v("miss", lo, 20), v("miss", 40 + lo, 60), scale=IRS)
    scan(v("sc", 0, 256), v("k320", 0, 256), v("vv", 0, 256), OP.min, OP.max, -H)
    ts(C0, KQ, 0.0, OP.is_equal, 40.0, OP.mult)
    below(15)
    tt(row(20, C), bank(6, 0, C), v("sc"), OP.is_le)
    below(14)
    scan(v("dsc"), v("kb"), row(20, C))
    below(13)
    tt(YY, v("m16"), v("dsc", 15, C, 16), OP.subtract)
    below(12)
    count(3)
    below(11)
    below(10)
    act(YI, YY, scale=IRS)
    below(9)
    count(4)
    below(8)
    count(2)
    for m in (7, 6, 5, 4):
        below(m)
    count(1)
    for m in (3, 2, 1):
        below(m)
    scan(v("rs", 128, C), v("kr", 128, C), bank(0, 0, 192))
    count(0)
    act(SO, SO, scale=4.0)
    act(v("k4", 0, NT), v("n4", 0, NT), AF.Sign)
    ts(v("me"), v("n4"), QQ, OP.is_equal, 4.0, OP.mult)
    tt(XX, YI, v("miss", 0, 20), OP.subtract)
    scan(v("rs", 0, 128), v("kr", 0, 128), bank(1, 0, 128))
    ts(v("so16"), v("so"), SO, OP.add)
    tt(TA, v("rs", 15, C, 16), XX, OP.add)
    ts(C1, KQ, 1.0, OP.is_equal, 80.0, OP.mult)
    ts(v("rk16"), TA, RS, OP.mult, CQ, OP.add)
    add("V", lambda q: q.tensor_copy(ap(v("orep")).indirect(ap(v("rk16"))), ap(v("c320"))), [v("rk16"), v("c320")], [v("orep")])
    act(v("s1"), bank(5, 0, C), AF.Copy)
    fill(v("tt", 320, 512), 0.0)
    affine([(BH, H_, BIG, 0.0), (BN, H_, -BIG, BIG), (pf(36, 4), v("me", 0, 4), BIG / 4, 0.0),
            (pf(40, 4), v("me", 0, 4), -BIG / 4, BIG), (S1K, H_, -1.0 / ZM, 0.0), (B1K, H_, -4.0, 1.0),
            (S3K, H_, -1.0, 1.0), (B3K, H_, 1.0 - ZB, ZB), (TH1, H_, -7.0, 8.0)])
    for j, c in enumerate([BH, MB[1], BN, MB[3]]):
        fill(four("hi", j), c)
    tt(v("g400", 0, NT), v("orep"), v("me", 0, NT), OP.mult, off=v("so16", 0, 5))
    scan(v("pp", 0, NT), v("k4", 0, NT), v("g400", 0, NT))
    ts(v("w16"), pj(0), T_, OP.add)

    def make_t(t, between=None):
        s, f = (z(0), 1.0) if t == 0 else (v("x32"), 2.0 ** -5)
        act(v("tt", 160, 320), s, AF.Copy, scale=f, off=v("w16", 10, 20))
        ts(v("tt", 0, 160), s, f, OP.mult, off=v("w16", 0, 10))
        if between:
            between()
        quant(v("qt%d" % t), v("st%d" % t), v("tt"))
        a, b = v("qt%d" % t, 0, NT), v("st%d" % t, 0, NT)
        send(u8(v("qx%d" % t, C, C + NT)), u8(a), [a], nxt, "ar%d" % t)
        send(ap(v("sx%d" % t, C, C + NT)), ap(b), [b], nxt, "ar%d" % t)

    def held_table(t, k0, k1, first, kh):
        act(U0, k0, AF.Abs, scale=-1.0, bias=KQ)
        act(U1, k1, AF.Abs, scale=-1.0, bias=KQ)
        act(first, U0, AF.Relu, scale=-40.0 * (2 * t + 1), bias=40.0 * (2 * t + 1))
        for j in (0, 2):
            act(kk(kh, j), U1, AF.Relu, scale=-40.0 * (2 * t + 2), bias=40.0 * (2 * t + 2))

    def places(p):
        affine([(four("ko", 1), p, S1K, B1K), (four("ko", 3), p, S3K, B3K)])

    def waits_for(d, js):
        affine([(four("hi", j), d, MS[j], [BH, MB[1], BN, MB[3]][j]) for j in js])

    def steps(k, code):
        for j in (1, 2, 3):
            ts(aa(k, j), code, TH[4 - j], OP.is_ge)

    def limits():
        tt(v("th"), v("bg", 0, C, 4), v("hi"), OP.subtract)

    def flight0():
        act(v("bg"), v("s1"), AF.Copy, off=v("b16"))
        act(kk(KC1, 3), pj(0), bias=T_)
        tt(v("g400", NT, 400), v("orep"), v("me", NT, 400), OP.mult, off=v("so16", 6, 26))
        act(v("k4", NT, 400), v("n4", NT, 400), AF.Sign)
        act(v("xph"), z(0), AF.Copy, scale=0.5, off=v("w16"))
        for b in range(4):
            a = 528 * (b % 2) + 2 - 2 * (b // 2)
            quant(v("qe", 128 * b, 128 * b + 128), v("se", 128 * b, 128 * b + 128), v("et", a, a + 512))
        limits()
        scan(v("pp", NT, 400), v("k4", NT, 400), v("g400", NT, 400))
        quant(v("qv"), v("sv"), v("vt"))
        tt(v("dp"), v("pp", NT + 3, 400, 4), v("pp", 3, C, 4), OP.subtract)
        places(kk(KC1, 3))
        affine([(four("ko", 2), four("hi", 0), 1.25 / BIG, -0.25), (four("kc", 2), four("hi", 0), -8.0 / BIG, 8.0),
                (four("kc", 3), four("hi", 0), 1.0 / BIG, 1.0), (CM, H_, -ZM - 2.0, 2.0), (CA, H_, ZB + 2.0, -ZB - 1.75),
                (pf(32, 3), v("c320", 1, 4), TH1, 0.0), (NI, I_, -1.0, 1.0)])
        whole(v("tab", 0, 40), -1)
        iota(v("tab", 40, 280), [[80, 3], [1, 2], [2, 40]])
        for k, j in ((KK0, 0), (KK1, 0), (KK1, 2)):
            whole(kk(k, j), 1)

    def flight(t):
        oc_, ow = (OC1, OW1) if t == 1 else (OC2, OW2)
        act(z(t, 2, 1280, 4), v("x32", 2, 1280, 4), AF.Copy, scale=2.0 ** -5)
        cp(v("x16"), oo(oc_, 3))
        ts(z(t, 3, 1280, 4), v("x32", 3, 1280, 4), 2.0 ** -5, OP.mult)
        scan(oo(ow), aa(t), kk(KW1 if t == 1 else KW2))
        act(v("xph"), v("x32"), AF.Copy, scale=2.0 ** -6, off=v("x16"))
        for k in range(2):
            a, b = hc * k, hc * k + hc
            quant(v("qx%d" % t, a, b), v("sx%d" % t, a, b), z(t, 4 * a, 4 * b))
            mm(bank(5 + k, 0, hc), UR[0], UR[1], v("qx%d" % t, a, b), v("sx%d" % t, a, b))
        ts(v("b16"), oo(ow, 3), T_, OP.subtract, 0.25, OP.mult)
        if t == 1:
            tt(F_, aa(A0, 3), aa(A0, 2), OP.subtract)
            scan(oo(OX1N), aa(AN0), kk(KX1))
            scan(oo(OX1), aa(A0), kk(KX1))
            d, js = D1, (1, 3)
        else:
            scan(oo(OD2), aa(A1), kk(KD2))
            scan(oo(OK0), aa(A1), kk(KK0))
            scan(oo(OK1), aa(A1), kk(KK1))
            d, js = oo(OD2, 3), (0, 1, 2, 3)
        act(v("s1", 0, hc), bank(5, 0, hc), AF.Copy)
        cp(v("s1", hc, C), bank(6, 0, hc))
        if t == 1:
            act(D1, F_, scale=SB)
            scan(oo(OX2N), aa(AN0), kk(KX2))
        else:
            tt(TD, LB, d, OP.subtract)
        act(v("bg", hc, C), v("s1"), AF.Copy, off=v("b16", 10, 20))
        cp(v("bg", 0, hc), v("s1"), off=v("b16", 0, 10))
        waits_for(d, js)
        places(oo(oc_, 3))
        if t == 1:
            tt(TD, LB, d, OP.subtract)
            scan(oo(OX2), aa(A0), kk(KX2))
        else:
            tt(kk(KH1, 1), V0_, kk(KH1, 0), OP.subtract)
            scan(oo(OH0), aa(A0), kk(KH0))
        ts(v("s16"), TD, float(C * t), OP.add)
        limits()

    make_t(0, lambda: ts(v("b16"), pj(0), 0.25, OP.mult))
    flight0()
    for t in range(R):
        last = t == R - 1
        arrive([v("qx%d" % t, C, C + NT), v("sx%d" % t, C, C + NT)], "ar%d" % t, 2 * prv[4])
        mq, msc = v("qx%d" % t, 272, 400), v("sx%d" % t, 272, 400)
        mm(bank(4, 0, 128), UR[0], UR[1], mq, msc)
        for b in range(4):
            mm(bank(b, 0, 128), v("qe", 128 * b, 128 * b + 128), v("se", 128 * b, 128 * b + 128), mq, msc)

        def keep():
            for b in range(4):
                acp(v("kept", C * t + b, C * t + C, 4), bank(b, 48, 128))

        if t:
            keep()
        code = v("cd", 3, NT, 4)
        lst = v("ls%d" % min(t, 1), 0, 20)
        tt(v("acc", NT, 2 * NT), bank(4, 48, 128), v("th"), OP.is_ge)
        tt(v("acc", 0, NT), bank(4, 48, 128), v("bg", 0, C, 4), OP.is_ge)
        scan(v("cd", NT, 2 * NT), v("ko"), v("acc", NT, 2 * NT))
        scan(v("cd", 0, NT), v("kc"), v("acc", 0, NT))
        ts(v("o16"), v("cd", NT + 3, 2 * NT, 4), CM, OP.mult, CA, OP.add)
        if t == 0:
            acp(lst, code)
        if t == 1:
            cp(lst, code)
        if not last:
            send(ap(v("lr%d" % t, 0, 20)), ap(lst), [lst], prv, "li%d" % t)
        if t == 0:
            for b in range(4):
                tt(v("bl", b, C, 4), bank(b, 48, 128), v("xph", b, C, 4), OP.add)
            acp(kk(KW1, 0), dpj(1))
            affine([(kk(KW1, 1), dpj(0), NI, 0.0), (kk(KW1, 2), dpj(0), I_, 0.0)])
            acp(kk(KW1, 3), kk(KC1, 3))
            keep()
            for k, j, s in ((KC1, 0, 1), (KC1, 1, 0), (KX1, 0, 2), (KX1, 2, 1), (KX2, 0, 3), (KX2, 2, 2), (KC3, 0, 3), (KC3, 1, 2)):
                acp(kk(k, j), dpj(s))
            for k, s in ((KX1, 1), (KX2, 2), (KC3, 2)):
                act(kk(k, 3), pj(s), bias=T_)
            affine([(SB, I_, 320.0, 0.0), (LB, v("m16"), 1.0, Q_)])
        else:
            if t == 1:
                tt(ln(8, 2), oo(OX1N, 3, 2), oo(OWN, 3, 2), OP.subtract)
                tt(kk(KW2N, 0, 2), oo(OX2N, 3, 2), oo(OX1N, 3, 2), OP.subtract)
            tt(v("bl"), v("kept", 0, C * t + C), v("xph"), OP.add, off=v("s16"))
        if t == 1:
            affine([(kk(KW2N, 1, 2), ln(8, 2), NI, 0.0), (kk(KW2N, 2, 2), ln(8, 2), I_, 0.0)])
            acp(kk(KW2N, 3, 2), oo(OWN, 3, 2))
            acp(kk(KC2, 3), oo(OC1, 3))
            affine([(SC_, I_, -320.0, 0.0), (SD, I_, -312.0, 316.0), (kk(KD2, 1), D1, -1.0, SC_), (kk(KD2, 0), F_, SD, 0.0),
                    (kk(KD2, 2), D1, -1.0, SB), (kk(KD2, 3), D1, 2.0, 0.0), (kk(KK0, 1), F_, 1.0, 1.0), (CDF, C1, -1.0, C0)])
            for j, c in ((0, C1), (2, C1), (1, CDF)):
                fill(kk(KH0, j), c)
            act(kk(KH0, 3), v("m16"), scale=0.125, bias=H_)
        if t == 2:
            acp(kk(KH1, 3), oo(OH0, 3))
            held_table(2, oo(OK0, 3), oo(OK1, 3), W0_, KH2)
        win = z(t, 0, ZW)
        add("V", lambda q, win=win: q.tensor_copy(ap(win).indirect(ap(v("o16"))), ap(v("bl"))), [v("o16"), v("bl")], [win])

        def layer(b, a, e, k):
            mm(bank(k, 0, e - a), v("qw", 128 * b, 128 * b + 128), v("sw", 128 * b, 128 * b + 128), v("qz", a, e), v("sz", a, e))

        def plus(b, a, e, k):
            tt(v("x32", 4 * a + b, 4 * e, 4), bank(k, 0, e - a), v("z32", C * b + a, C * b + e), OP.add)

        def back32(b):
            act(z(t + 1, b, 1280, 4), v("x32", b, 1280, 4), AF.Copy, scale=2.0 ** -5)

        parts = [(0, 0, hc, 6), (0, hc, C, 7), (1, hc, C, 1), (2, 0, C, 2), (3, 0, hc, 3), (3, hc, C, 0), (1, 0, hc, 4)]
        for k in range(2):
            quant(v("qz", hc * k, hc * k + hc), v("sz", hc * k, hc * k + hc), z(t, 4 * hc * k, 4 * hc * (k + 1)))
        for b in range(4):
            act(v("z32", C * b, C * b + C), z(t, b, 1280, 4), AF.Copy, scale=32.0)
        for k in (0, 6, 1, 2, 3, 4, 5):
            layer(*parts[k])
        steps(A0 + t, code)
        plus(*parts[0])
        plus(*parts[6])
        plus(*parts[1])
        back32(0)
        if not last:
            an, on, kn = (AN0, OWN, KW1) if t == 0 else (AN1, OWN2, KW2N)
            if t == 1:
                scan(oo(OC3), aa(A0), kk(KC3))
                tt(kk(KC2, 1), oo(OX1, 3), oo(OC1, 3), OP.subtract)
            plus(*parts[2])
            back32(1)
            arrive([v("lr%d" % t, 0, 20)], "li%d" % t, nxt[4])
            steps(an, v("lr%d" % t, 0, 20))
            plus(*parts[3])
            scan(oo(on), aa(an), kk(kn))
            if t == 1:
                tt(kk(KC2, 0), oo(OC3, 3), oo(OX1, 3), OP.subtract)
            plus(*parts[4])
            cp(v("w16"), oo(on, 3))
            plus(*parts[5])
            make_t(t + 1, lambda: scan(oo(OC1 if t == 0 else OC2), aa(A0 + t), kk(KC1 if t == 0 else KC2)))
            flight(t + 1)
            if t == 0:
                tt(K01, aa(A0, 2), aa(A0, 1), OP.add)
                tt(TA, aa(A0, 3), aa(A0, 1), OP.add)
                act(K11, TA, bias=1.0)
                acp(kk(KK0, 3), K01)
                act(kk(KK1, 3), TA, bias=1.0)
                held_table(1, K01, K11, V0_, KH1)
            continue

        scan(oo(OH1), aa(A1), kk(KH1))
        tt(kk(KH2, 1), W0_, kk(KH2, 0), OP.subtract)
        plus(*parts[2])
        back32(1)
        cp(kk(KH2, 3), oo(OH1, 3))
        plus(*parts[3])
        scan(oo(OH), aa(A2), kk(KH2))
        plus(*parts[4])
        cp(v("h16"), oo(OH, 3))
        act(v("skr"), v("tab"), AF.Copy, off=v("h16"))
        dma("A", T.sk[:, :], T.skr[0:128:16, :], [v("skr")], [], "o8")

        def back(b, k):
            a, e = 4 * hc * k + b, 4 * hc * (k + 1)
            ts(z(3, a, e, 4), v("x32", a, e, 4), 2.0 ** -5, OP.mult)

        def finish(k):
            a, e = hc * k, hc * k + hc
            quant(v("qx3", a, e), v("sx3", a, e), z(3, 4 * a, 4 * e))
            mm(bank(4 + k, 0, hc), v("qv"), v("sv"), v("qx3", a, e), v("sx3", a, e))
            dma("S", T.oc[:, 4 * a:4 * e], u8(v("qx3", a, e)), [v("qx3", a, e)], [], "o%d" % k)

        def result(k):
            r = v("yb", hc * k, hc * k + hc)
            cp(r, bank(4 + k, 0, hc))
            dma("S", T.y[:, hc * k:hc * k + hc], ap(r), [r], [], "o%d" % (6 + k))

        back(2, 0)
        back(3, 0)
        plus(*parts[5])
        back(2, 1)
        finish(0)
        back(3, 1)
        finish(1)
        for k in range(4):
            dma("A", T.osc[4 * k:4 * k + 4, :], T.sx3[32 * k:32 * k + 4, :], [v("sx3")], [], "o%d" % (2 + k))
        result(0)
        result(1)
    return ops


def meets(r, s):
    if r[0] != s[0]:
        return False
    if r[0] == "ps":
        return r[1] // 512 == s[1] // 512
    if r[2] <= s[1] or s[2] <= r[1]:
        return False
    if r[3] == 1 and s[3] == 1:
        return True
    return len(set(range(r[1], r[2], r[3])) & set(range(s[1], s[2], s[3]))) > 0


def order(ops):
    seen = {}
    deps = []
    for n, o in enumerate(ops):
        d = set()
        for r, w in [(r, False) for r in o["rd"]] + [(r, True) for r in o["wr"]]:
            for (m, s, w2) in seen.get(r[0], []):
                other = ops[m]["e"] != o["e"]
                if (w or w2 or (r[0] == "ps" and other)) and meets(r, s) and not (o["acc"] and not other):
                    d.add(m)
        for r, w in [(r, False) for r in o["rd"]] + [(r, True) for r in o["wr"]]:
            seen.setdefault(r[0], []).append((n, r, w))
        deps.append(d if o["kind"] != "arrive" else set())
    return deps


def plan(ops):
    deps = order(ops)
    place, cnt = {}, {}
    for n, o in enumerate(ops):
        if o["kind"] == "op":
            cnt[o["e"]] = cnt.get(o["e"], 0) + 1
            place[n] = (o["e"], cnt[o["e"]])
        elif o["kind"] in ("dma", "arrive"):
            place[n] = (o["sem"], 1)
    know, at, waits = {}, [], []
    for n, o in enumerate(ops):
        k = know.setdefault(o["e"], {})
        w = []
        for m in sorted(deps[n], reverse=True):
            key, c = place[m]
            if k.get(key, 0) >= c:
                continue
            w.append(m)
            k[key] = c
            for key2, c2 in at[m].items():
                if k.get(key2, 0) < c2:
                    k[key2] = c2
        waits.append(w)
        at.append(dict(k))
    return waits


def rank_program(g, core, T, topo):
    rank = T.rank_of(core)
    if rank is None:
        return
    n = len(T.cores)
    cn, cp_, cnn = T.cores[(rank + 1) % n], T.cores[(rank - 1) % n], T.cores[(rank + 2) % n]

    def back(a, b, c):
        return topo.mask(a, b) & topo.mask(a, c)

    def bits(m):
        return bin(m).count("1")

    rn, pn = topo.addr(cn, core)
    rp, pp_ = topo.addr(cp_, core)
    nxt = (rn, pn, topo.mask(core, cn), bits(topo.mask(core, cn)), bits(back(cn, core, cnn)))
    prv = (rp, pp_, back(core, cp_, cn), bits(back(core, cp_, cn)), bits(topo.mask(cp_, core)))
    ops = build(T, nxt, prv)
    waits = plan(ops)
    needed = set(m for w in waits for m in w)
    queue = {"V": g.vector, "A": g.scalar, "P": g.tensor, "G": g, "S": g.sync}
    last = {}
    for k, o in enumerate(ops):
        if o["kind"] == "op":
            last[o["e"]] = k
    value, total, sent = {}, {}, 0
    for k, o in enumerate(ops):
        if o["kind"] == "op" and (k in needed or last[o["e"]] == k):
            total[o["e"]] = total.get(o["e"], 0) + 1
            value[k] = (ENG_SEM[o["e"]], total[o["e"]])
        elif o["kind"] in ("dma", "arrive"):
            value[k] = (o["sem"], o["cnt"])
    for k, o in enumerate(ops):
        if o["kind"] == "arrive":
            continue
        q = queue[o["e"]]
        for m in waits[k]:
            q.wait_ge(T.sem[value[m][0]], value[m][1])
        ins = o["fn"](q)
        if o["kind"] == "dma":
            ins.then_inc(T.sem[o["sem"]], 16)
        elif o["kind"] == "send":
            sent += o["cnt"]
        elif k in value:
            ins.then_inc(T.sem[value[k][0]], 1)
    g.wait_ge(T.sem["loc"], sent)
    for e, c in total.items():
        g.wait_ge(T.sem[ENG_SEM[e]], c)
    for k, o in enumerate(ops):
        if o["kind"] in ("dma", "arrive"):
            g.wait_ge(T.sem[o["sem"]], o["cnt"])
